import numpy as np
import ml_dtypes


def mxq(x, axis, fmt="e4m3"):
    dtype, down = {"e4m3": (ml_dtypes.float8_e4m3fn, 7), "e5m2": (ml_dtypes.float8_e5m2, 14)}[fmt]
    v = np.moveaxis(np.asarray(x, np.float32).astype(ml_dtypes.bfloat16).astype(np.float64), axis, -1)
    blocks = v.reshape(v.shape[:-1] + (-1, 32))
    amax = np.abs(blocks).max(-1, keepdims=True)
    byte = np.maximum(np.where(amax > 0, np.frexp(amax)[1] - 1 + 127, 0) - down, 1)
    scale = np.exp2(byte - 127.0)
    codes = (blocks / scale).astype(np.float32).astype(dtype).astype(np.float64)
    return np.moveaxis((codes * scale).reshape(v.shape), -1, axis)


WIDE = False


def mx_kscale(k):
    if not WIDE:
        return np.ones(k)
    levels = np.array([24, -24, 12, -12, 0])
    if k % 512:
        return np.exp2(np.random.permutation(np.resize(levels, k // 32))).repeat(32)
    a = np.empty((k // 512, 16))
    for p in range(k // 512):
        a[p, :8] = np.random.permutation(np.resize(levels, 8))
        for g in range(8):
            far = levels[np.abs(levels - a[p, g]) >= 10]
            a[p, g + 8] = far[np.random.randint(len(far))]
    return np.exp2(a.ravel()).repeat(32)


def f64(x):
    return np.asarray(x).astype(np.float64)


def striped(idx):
    return np.tile(idx.reshape(-1, 16).T, (8, 1)).astype(np.uint16)


def unstriped(offs):
    return offs[:16].T.reshape(-1).astype(np.int64)


E2M1 = np.array([0.0, 0.5, 1.0, 1.5, 2.0, 3.0, 4.0, 6.0, -0.0, -0.5, -1.0, -1.5, -2.0, -3.0, -4.0, -6.0])


def pack_weight(w, fmt):
    k, n = w.shape
    w = f64(np.asarray(w, np.float32).astype(ml_dtypes.bfloat16)).reshape(k // 32, 32, n)
    amax = np.abs(w).max(1)
    if fmt == "e4m3":
        byte = np.frexp(amax)[1] - 1 + 127 - 7
    else:
        mant, ex = np.frexp(amax / 6.0)
        byte = np.where(mant > 0.5, ex, ex - 1) + 127
    byte = np.clip(np.where(amax > 0, byte, 1), 1, 254)
    scaled = (w * np.exp2(127.0 - byte)[:, None, :]).reshape(k, n).astype(np.float32)
    by_word = np.ascontiguousarray(scaled.reshape(k // 512, 128, 4, n).transpose(0, 1, 3, 2))
    if fmt == "e4m3":
        words = by_word.astype(ml_dtypes.float8_e4m3fn).view(np.uint8)
    else:
        c = by_word.astype(ml_dtypes.float4_e2m1fn).view(np.uint8) & 0xF
        words = (c[..., 0::2] | (c[..., 1::2] << 4)).reshape(k // 512, 128, 2 * n)
    return np.ascontiguousarray(words), np.ascontiguousarray(byte.astype(np.uint8).reshape(k // 512, 16, n))


def unpack_weight(words, scales, fmt):
    g, _, n = scales.shape
    words = np.ascontiguousarray(words).reshape(g, 128, n, -1)
    if fmt == "e4m3":
        vals = words.view(ml_dtypes.float8_e4m3fn).astype(np.float64)
    else:
        nib = np.empty((g, 128, n, 4), np.uint8)
        nib[..., 0::2] = words & 0xF
        nib[..., 1::2] = words >> 4
        vals = E2M1[nib]
    vals = vals * np.repeat(np.exp2(scales.astype(np.float64) - 127.0), 8, axis=1)[..., None]
    return vals.transpose(0, 1, 3, 2).reshape(g * 512, n)


K, R, N, T, J = 512, 1024, 256, 2048, 512


def setup_inputs():
    n = np.random.standard_normal
    s = mx_kscale(K)[:, None]
    u = mx_kscale(R)[:, None]
    wd = n((R, N)) / np.sqrt(R) / u
    p_tab = pack_weight(n((K, T)) * s, "e4m3")
    p_w = pack_weight(n((K, R)) / np.sqrt(K) / s * u.T, "e4m3")
    p_wd8 = pack_weight(wd[:512], "e4m3")
    p_wd4 = pack_weight(wd[512:], "e2m1")
    return {
        "tab_words": p_tab[0],
        "tab_scales": p_tab[1],
        "c": (n((K, J)) * s).astype(np.float32),
        "w_words": p_w[0],
        "w_scales": p_w[1],
        "wc": (n((K, R)) / np.sqrt(K) / s * u.T).astype(np.float32),
        "wd8_words": p_wd8[0],
        "wd8_scales": p_wd8[1],
        "wd4_words": p_wd4[0],
        "wd4_scales": p_wd4[1],
        "offs": striped(np.concatenate([np.random.permutation(T)[:J] for _ in range(4)])),
    }


def reference(tab_words, tab_scales, c, w_words, w_scales, wc, wd8_words, wd8_scales, wd4_words, wd4_scales, offs):
    idx = unstriped(offs).reshape(4, J)
    tab_ = unpack_weight(tab_words, tab_scales, "e4m3")[:, idx]
    c_ = mxq(f64(c), 0, "e4m3")
    w_ = unpack_weight(w_words, w_scales, "e4m3")
    a0 = w_.T @ tab_[:, 0]
    a1 = w_.T @ tab_[:, 1]
    a2 = w_.T @ tab_[:, 2]
    a3 = w_.T @ tab_[:, 3]
    wc_ = mxq(f64(wc), 0, "e4m3")
    ac = wc_.T @ c_
    h = np.maximum(np.maximum(np.maximum(np.maximum(a0, a1), a2), a3) + ac, 0.0)
    h_ = mxq(h, 0, "e4m3")
    wd8_ = unpack_weight(wd8_words, wd8_scales, "e4m3")
    wd4_ = unpack_weight(wd4_words, wd4_scales, "e2m1")
    y = wd8_.T @ h_[:512] + wd4_.T @ h_[512:]
    return y

@@ -1,0 +1,261 @@
+from contextlib import ExitStack
+
+import concourse.mybir as mybir
+from concourse.masks import make_identity
+
+K, R, N, T, J, G = 512, 1024, 256, 2048, 512, 4
+FLOPS = 2 * K * R * J * (G + 1) + 2 * R * N * J
+
+F32 = mybir.dt.float32
+BF16 = mybir.dt.bfloat16
+I32 = mybir.dt.int32
+U32 = mybir.dt.uint32
+U16 = mybir.dt.uint16
+U8 = mybir.dt.uint8
+FP8X4 = mybir.dt.float8_e4m3fn_x4
+FP4X4 = mybir.dt.float4_e2m1fn_x4
+ALU = mybir.AluOpType
+ACT = mybir.ActivationFunctionType
+
+P = 128
+PACK = 4
+BANK = 512
+JT = J // P
+RH = R // BANK
+UNITS = JT * RH
+LIST_COLS = J // 16
+
+
+def load_scale_rows(queue, plane, rows):
+    for q in range(4):
+        queue.dma_start(out=plane[32 * q : 32 * q + 4, :], in_=rows[4 * q : 4 * q + 4, :].bitcast(I32))
+
+
+def tile_list_pnet_mix_none_kernel(
+    tc, tab_words, tab_scales, c, w_words, w_scales, wc, wd8_words, wd8_scales, wd4_words, wd4_scales, offs, out
+):
+    nc = tc.nc
+    with ExitStack() as ctx:
+        keep = ctx.enter_context(tc.tile_pool(name="keep", bufs=1))
+        ring = ctx.enter_context(tc.tile_pool(name="ring", bufs=4))
+        ps_s = ctx.enter_context(tc.psum_pool(name="ps_s", bufs=2))
+        ps_t = ctx.enter_context(tc.psum_pool(name="ps_t", bufs=1))
+        ps_v = ctx.enter_context(tc.psum_pool(name="ps_v", bufs=5))
+
+        offsets = keep.tile([P, G * LIST_COLS], U16, name="offsets")
+        tab_sc = keep.tile([P, T // 4], I32, name="tab_sc", align_bytes=64)
+        w_sc = keep.tile([P, R // 4], I32, name="w_sc", align_bytes=64)
+        wd8_sc = keep.tile([P, N // 4], I32, name="wd8_sc", align_bytes=64)
+        wd4_sc = keep.tile([P, N // 4], I32, name="wd4_sc", align_bytes=64)
+        tab_w = keep.tile([P, T], U32, name="tab_w", align_bytes=64)
+        w_w = keep.tile([P, R], U32, name="w_w", align_bytes=64)
+        wd8_w = keep.tile([P, N], U32, name="wd8_w", align_bytes=64)
+        wd4_w = keep.tile([P, 2 * N], U8, name="wd4_w", align_bytes=64)
+        ident = keep.tile([P, P], BF16, name="ident")
+
+        nc.vector.memset(tab_sc[:, : T // 8], 0)
+        nc.gpsimd.memset(tab_sc[:, T // 8 :], 0)
+        nc.vector.memset(w_sc[:], 0)
+        nc.vector.memset(wd8_sc[:], 0)
+        nc.vector.memset(wd4_sc[:], 0)
+        make_identity(nc, ident[:])
+        c_raw = keep.tile([P, PACK, J], F32, name="c_raw", tag="stage_c")
+        wc_raw = [keep.tile([P, PACK, BANK], F32, name=f"wc_raw{h}", tag=f"stage_wc{h}") for h in range(RH)]
+
+        nc.sync.dma_start(offsets[:], offs)
+        load_scale_rows(nc.sync, tab_sc, tab_scales[0])
+        nc.sync.dma_start(out=wd4_w[:].bitcast(I32), in_=wd4_words[0].bitcast(I32))
+        nc.sync.dma_start(out=tab_w[:].bitcast(I32), in_=tab_words[0].rearrange("p t i -> p (t i)").bitcast(I32))
+        nc.sync.dma_start(out=w_w[:].bitcast(I32), in_=w_words[0].rearrange("p r i -> p (r i)").bitcast(I32))
+        load_scale_rows(nc.sync, w_sc, w_scales[0])
+        nc.sync.dma_start(out=c_raw[:], in_=c.rearrange("(p i) j -> p i j", i=PACK))
+        for h in range(RH):
+            nc.sync.dma_start(
+                out=wc_raw[h][:], in_=wc[:, h * BANK : (h + 1) * BANK].rearrange("(p i) r -> p i r", i=PACK)
+            )
+        load_scale_rows(nc.sync, wd8_sc, wd8_scales[0])
+        load_scale_rows(nc.sync, wd4_sc, wd4_scales[0])
+        nc.sync.dma_start(out=wd8_w[:].bitcast(I32), in_=wd8_words[0].rearrange("p n i -> p (n i)").bitcast(I32))
+
+        nb_w = [keep.tile([P, J], U32, name=f"nb_w{g}", align_bytes=64) for g in range(G)]
+        nb_sc = [keep.tile([P, 2 * J], U8, name=f"nb_sc{g2}", align_bytes=64) for g2 in range(G // 2)]
+        for g2 in range(G // 2):
+            nc.vector.tensor_copy(
+                nb_sc[g2][:],
+                tab_sc[:].bitcast(U8).indirect(offsets[:, 2 * g2 * LIST_COLS : 2 * (g2 + 1) * LIST_COLS]),
+            )
+            for g in (2 * g2, 2 * g2 + 1):
+                nc.vector.tensor_copy(
+                    nb_w[g][:], tab_w[:].indirect(offsets[:, g * LIST_COLS : (g + 1) * LIST_COLS])
+                )
+
+        c_w = keep.tile([P, J], U32, name="c_w", align_bytes=64)
+        c_sc = keep.tile([P, J], U8, name="c_sc", align_bytes=64)
+        wc_w = [keep.tile([P, BANK], U32, name=f"wc_w{h}", align_bytes=64) for h in range(RH)]
+        wc_sc = [keep.tile([P, BANK], U8, name=f"wc_sc{h}", align_bytes=64) for h in range(RH)]
+
+        def quantise(raw, words, scales, name, on_gpsimd):
+            grouped = keep.tile([P, BANK, PACK], BF16, name=name, align_bytes=64)
+            if on_gpsimd:
+                for s in range(4):
+                    cols = slice(s * P, (s + 1) * P)
+                    nc.gpsimd.tensor_scalar(
+                        grouped[:, cols, :],
+                        raw[:, :, cols].rearrange("p i a -> p a i"),
+                        1.0,
+                        0.0,
+                        ALU.mult,
+                        ALU.add,
+                    )
+            else:
+                nc.scalar.activation(
+                    grouped[:].rearrange("p (a b) i -> p a i b", b=4),
+                    raw[:].rearrange("p i (a b) -> p a i b", b=4),
+                    ACT.Copy,
+                )
+            nc.vector.quantize_mx(
+                out=words[:].bitcast(FP8X4), scales=scales[:], in_=grouped[:].rearrange("p a i -> p (a i)")
+            )
+
+        def nb_pass(bank, u, g, start, stop):
+            h, jt = divmod(u, JT)
+            nc.tensor.matmul_mx(
+                out=bank[:],
+                lhsT=nb_w[g][:, jt * P : (jt + 1) * P].bitcast(FP8X4),
+                lhsT_scale=nb_sc[g // 2][:, (g % 2) * J + jt * P : (g % 2) * J + (jt + 1) * P],
+                rhs=w_w[:, h * BANK : (h + 1) * BANK].bitcast(FP8X4),
+                rhs_scale=w_sc[:].bitcast(U8)[:, h * BANK : (h + 1) * BANK],
+                start=start,
+                stop=stop,
+            )
+
+        def own_pass(bank, u, start, stop):
+            h, jt = divmod(u, JT)
+            nc.tensor.matmul_mx(
+                out=bank[:],
+                lhsT=c_w[:, jt * P : (jt + 1) * P].bitcast(FP8X4),
+                lhsT_scale=c_sc[:, jt * P : (jt + 1) * P],
+                rhs=wc_w[h][:].bitcast(FP8X4),
+                rhs_scale=wc_sc[h][:],
+                start=start,
+                stop=stop,
+            )
+
+        def by_slot(bank):
+            return bank[:].rearrange("j (p t) -> j t p", t=PACK)
+
+        LAST = UNITS - 1
+        pooled = {}
+
+        def claim(units, tag):
+            shared = keep.tile([P, len(units), PACK, P], F32, name=f"pooled_{tag}", tag=tag)
+            for i, u in enumerate(units):
+                pooled[u] = shared[:, i, :, :]
+
+        summed = {}
+        h_bf = [keep.tile([P, J, PACK], BF16, name=f"h_bf{h}", align_bytes=64) for h in range(RH)]
+        h_w = [keep.tile([P, J], U32, name=f"h_w{h}", align_bytes=64) for h in range(RH)]
+        h_sc = [keep.tile([P, J], U8, name=f"h_sc{h}", align_bytes=64) for h in range(RH)]
+
+        def neighbour(u, g):
+            bank = (ps_s if g == 0 else ps_v).tile([P, BANK], F32, name="bank", tag="bank")
+            if u == LAST:
+                own_pass(bank, u, True, False)
+                nb_pass(bank, u, g, False, True)
+            else:
+                nb_pass(bank, u, g, True, True)
+            if g == 0:
+                nc.scalar.activation(pooled[u], by_slot(bank), ACT.Copy)
+            elif u == LAST and g == G - 1:
+                summed[u] = ring.tile([P, PACK, P], BF16, name="summed")
+                nc.vector.scalar_tensor_tensor(summed[u][:], by_slot(bank), 0.0, pooled[u], ALU.max, ALU.max)
+            else:
+                nc.vector.tensor_tensor(pooled[u], by_slot(bank), pooled[u], ALU.max)
+
+        own = [keep.tile([P, PACK, P], F32, name=f"own{u}") for u in range(LAST)]
+
+        def own_part(u):
+            bank = ps_s.tile([P, BANK], F32, name="bank", tag="bank")
+            own_pass(bank, u, True, True)
+            nc.scalar.activation(own[u][:], by_slot(bank), ACT.Copy)
+
+        def finish(u):
+            h, jt = divmod(u, JT)
+            if u != LAST:
+                summed[u] = ring.tile([P, PACK, P], BF16, name="summed")
+                nc.gpsimd.tensor_tensor(summed[u][:], pooled[u], own[u][:], ALU.add)
+            if u in (5, 7):
+                turned = ps_s.tile([P, PACK, P], BF16, name="turned", tag="bank")
+            else:
+                turned = ps_t.tile([P, PACK, P], BF16, name="turned")
+            for t in range(PACK):
+                nc.tensor.transpose(turned[:, t, :], summed[u][:, t, :], ident[:])
+            nc.scalar.activation(h_bf[h][:, jt * P : (jt + 1) * P, :], turned[:].rearrange("p t j -> p j t"), ACT.Relu)
+
+        def quantise_h(h, points):
+            nc.vector.quantize_mx(
+                out=h_w[h][:, points].bitcast(FP8X4),
+                scales=h_sc[h][:, points],
+                in_=h_bf[h][:, points, :].rearrange("p j t -> p (j t)"),
+            )
+
+        def second_layer(jt):
+            points = slice(jt * P, (jt + 1) * P)
+            quantise_h(1, points)
+            y = ps_v.tile([P, N // P, P], F32, name="y", tag="bank")
+            for nt in range(N // P):
+                nc.tensor.matmul_mx(
+                    out=y[:, nt, :],
+                    lhsT=wd8_w[:, nt * P : (nt + 1) * P].bitcast(FP8X4),
+                    lhsT_scale=wd8_sc[:].bitcast(U8)[:, nt * P : (nt + 1) * P],
+                    rhs=h_w[0][:, points].bitcast(FP8X4),
+                    rhs_scale=h_sc[0][:, points],
+                    start=True,
+                    stop=False,
+                )
+                nc.tensor.matmul_mx(
+                    out=y[:, nt, :],
+                    lhsT=wd4_w[:, 2 * nt * P : 2 * (nt + 1) * P].bitcast(FP4X4),
+                    lhsT_scale=wd4_sc[:].bitcast(U8)[:, nt * P : (nt + 1) * P],
+                    rhs=h_w[1][:, points].bitcast(FP8X4),
+                    rhs_scale=h_sc[1][:, points],
+                    start=False,
+                    stop=True,
+                )
+            y_sb = ring.tile([P, N // P, P], F32, name="y_sb")
+            if jt % 2 == 0:
+                nc.vector.tensor_copy(y_sb[:], y[:])
+            else:
+                nc.scalar.activation(y_sb[:], y[:], ACT.Copy)
+            nc.sync.dma_start(
+                out=out[:, jt * P : (jt + 1) * P].rearrange("(nt n) j -> n nt j", n=P), in_=y_sb[:]
+            )
+
+        EARLY = 4
+        quantise(c_raw, c_w, c_sc, "c_bf", False)
+        claim([0, 1], "stage_c")
+        neighbour(0, 0)
+        neighbour(1, 0)
+        quantise(wc_raw[0], wc_w[0], wc_sc[0], "wc_bf0", False)
+        claim([2, 3], "stage_wc0")
+        neighbour(2, 0)
+        neighbour(3, 0)
+        quantise(wc_raw[1], wc_w[1], wc_sc[1], "wc_bf1", True)
+        claim([4, 5, 6, 7], "stage_wc1")
+        for u in range(UNITS + 1):
+            if u < LAST:
+                own_part(u)
+            if u + EARLY < UNITS:
+                neighbour(u + EARLY, 0)
+            if u < UNITS:
+                neighbour(u, 1)
+            if u >= 1:
+                neighbour(u - 1, 3)
+            if u < UNITS:
+                neighbour(u, 2)
+            if u >= 2:
+                finish(u - 2)
+        finish(LAST)
+        quantise_h(0, slice(0, J))
+        for jt in range(JT):
+            second_layer(jt)

@@ -51,7 +51,7 @@ def tile_list_pnet_mix_none_kernel(
         w_w = keep.tile([P, R], U32, name="w_w", align_bytes=64)
         wd8_w = keep.tile([P, N], U32, name="wd8_w", align_bytes=64)
         wd4_w = keep.tile([P, 2 * N], U8, name="wd4_w", align_bytes=64)
-        ident = keep.tile([P, P], BF16, name="ident")
+        ident = keep.tile([P, P], F32, name="ident")
 
         nc.vector.memset(tab_sc[:, : T // 8], 0)
         nc.gpsimd.memset(tab_sc[:, T // 8 :], 0)
@@ -65,10 +65,10 @@ def tile_list_pnet_mix_none_kernel(
         nc.sync.dma_start(offsets[:], offs)
         load_scale_rows(nc.sync, tab_sc, tab_scales[0])
         nc.sync.dma_start(out=wd4_w[:].bitcast(I32), in_=wd4_words[0].bitcast(I32))
+        nc.sync.dma_start(out=c_raw[:], in_=c.rearrange("(p i) j -> p i j", i=PACK))
         nc.sync.dma_start(out=tab_w[:].bitcast(I32), in_=tab_words[0].rearrange("p t i -> p (t i)").bitcast(I32))
         nc.sync.dma_start(out=w_w[:].bitcast(I32), in_=w_words[0].rearrange("p r i -> p (r i)").bitcast(I32))
         load_scale_rows(nc.sync, w_sc, w_scales[0])
-        nc.sync.dma_start(out=c_raw[:], in_=c.rearrange("(p i) j -> p i j", i=PACK))
         for h in range(RH):
             nc.sync.dma_start(
                 out=wc_raw[h][:], in_=wc[:, h * BANK : (h + 1) * BANK].rearrange("(p i) r -> p i r", i=PACK)
@@ -141,16 +141,24 @@ def tile_list_pnet_mix_none_kernel(
                 stop=stop,
             )
 
-        def by_slot(bank):
+        ON_VECTOR = (6, 7)
+
+        def by_slot(bank, u):
+            if u in ON_VECTOR:
+                return bank[:].rearrange("j (p a e) -> j a p e", a=2, e=2)
             return bank[:].rearrange("j (p t) -> j t p", t=PACK)
 
-        LAST = UNITS - 1
+        def like_slot(flat, u):
+            if u in ON_VECTOR:
+                return flat.rearrange("j (a p e) -> j a p e", a=2, e=2)
+            return flat.rearrange("j (t p) -> j t p", t=PACK)
+
         pooled = {}
 
         def claim(units, tag):
-            shared = keep.tile([P, len(units), PACK, P], F32, name=f"pooled_{tag}", tag=tag)
+            shared = keep.tile([P, len(units), BANK], F32, name=f"pooled_{tag}", tag=tag)
             for i, u in enumerate(units):
-                pooled[u] = shared[:, i, :, :]
+                pooled[u] = shared[:, i, :]
 
         summed = {}
         h_bf = [keep.tile([P, J, PACK], BF16, name=f"h_bf{h}", align_bytes=64) for h in range(RH)]
@@ -159,38 +167,43 @@ def tile_list_pnet_mix_none_kernel(
 
         def neighbour(u, g):
             bank = (ps_s if g == 0 else ps_v).tile([P, BANK], F32, name="bank", tag="bank")
-            if u == LAST:
-                own_pass(bank, u, True, False)
-                nb_pass(bank, u, g, False, True)
-            else:
-                nb_pass(bank, u, g, True, True)
+            nb_pass(bank, u, g, True, True)
             if g == 0:
-                nc.scalar.activation(pooled[u], by_slot(bank), ACT.Copy)
-            elif u == LAST and g == G - 1:
-                summed[u] = ring.tile([P, PACK, P], BF16, name="summed")
-                nc.vector.scalar_tensor_tensor(summed[u][:], by_slot(bank), 0.0, pooled[u], ALU.max, ALU.max)
+                nc.scalar.activation(like_slot(pooled[u], u), by_slot(bank, u), ACT.Copy)
             else:
-                nc.vector.tensor_tensor(pooled[u], by_slot(bank), pooled[u], ALU.max)
+                nc.vector.tensor_tensor(like_slot(pooled[u], u), by_slot(bank, u), like_slot(pooled[u], u), ALU.max)
 
-        own = [keep.tile([P, PACK, P], F32, name=f"own{u}") for u in range(LAST)]
+        own = {u: keep.tile([P, BANK], F32, name=f"own{u}") for u in range(UNITS) if u not in ON_VECTOR}
 
         def own_part(u):
-            bank = ps_s.tile([P, BANK], F32, name="bank", tag="bank")
+            bank = (ps_v if u in ON_VECTOR else ps_s).tile([P, BANK], F32, name="bank", tag="bank")
             own_pass(bank, u, True, True)
-            nc.scalar.activation(own[u][:], by_slot(bank), ACT.Copy)
+            if u in ON_VECTOR:
+                summed[u] = ring.tile([P, BANK], BF16, name="summed")
+                nc.vector.tensor_tensor(like_slot(summed[u][:], u), by_slot(bank, u), like_slot(pooled[u], u), ALU.add)
+            else:
+                nc.scalar.activation(like_slot(own[u][:], u), by_slot(bank, u), ACT.Copy)
 
         def finish(u):
             h, jt = divmod(u, JT)
-            if u != LAST:
-                summed[u] = ring.tile([P, PACK, P], BF16, name="summed")
-                nc.gpsimd.tensor_tensor(summed[u][:], pooled[u], own[u][:], ALU.add)
-            if u in (5, 7):
-                turned = ps_s.tile([P, PACK, P], BF16, name="turned", tag="bank")
+            dst = h_bf[h][:, jt * P : (jt + 1) * P, :]
+            if u in ON_VECTOR:
+                turned = ps_s.tile([P, 2, P], F32, name="turned", tag="bank")
+                words = summed[u][:].bitcast(F32)
+                for a in range(2):
+                    nc.tensor.transpose(turned[:, a, :], words[:, a * P : (a + 1) * P], ident[:])
+                nc.scalar.activation(
+                    dst.rearrange("p j (a e) -> p j a e", e=2),
+                    turned[:].bitcast(BF16).rearrange("p a (j e) -> p j a e", e=2),
+                    ACT.Relu,
+                )
             else:
-                turned = ps_t.tile([P, PACK, P], BF16, name="turned")
-            for t in range(PACK):
-                nc.tensor.transpose(turned[:, t, :], summed[u][:, t, :], ident[:])
-            nc.scalar.activation(h_bf[h][:, jt * P : (jt + 1) * P, :], turned[:].rearrange("p t j -> p j t"), ACT.Relu)
+                turned = ps_t.tile([P, PACK, P], F32, name="turned")
+                for t in range(PACK):
+                    cols = slice(t * P, (t + 1) * P)
+                    nc.tensor.matmul(turned[:, t, :], own[u][:, cols], ident[:], start=True, stop=False, is_transpose=True)
+                    nc.tensor.matmul(turned[:, t, :], pooled[u][:, cols], ident[:], start=False, stop=True, is_transpose=True)
+                nc.scalar.activation(dst, turned[:].rearrange("p t j -> p j t"), ACT.Relu)
 
         def quantise_h(h, points):
             nc.vector.quantize_mx(
@@ -240,10 +253,10 @@ def tile_list_pnet_mix_none_kernel(
         claim([2, 3], "stage_wc0")
         neighbour(2, 0)
         neighbour(3, 0)
-        quantise(wc_raw[1], wc_w[1], wc_sc[1], "wc_bf1", True)
+        quantise(wc_raw[1], wc_w[1], wc_sc[1], "wc_bf1", False)
         claim([4, 5, 6, 7], "stage_wc1")
         for u in range(UNITS + 1):
-            if u < LAST:
+            if u < UNITS and u not in ON_VECTOR:
                 own_part(u)
             if u + EARLY < UNITS:
                 neighbour(u + EARLY, 0)
@@ -253,9 +266,11 @@ def tile_list_pnet_mix_none_kernel(
                 neighbour(u - 1, 3)
             if u < UNITS:
                 neighbour(u, 2)
+            if u - 1 in ON_VECTOR:
+                own_part(u - 1)
             if u >= 2:
                 finish(u - 2)
-        finish(LAST)
+        finish(UNITS - 1)
         quantise_h(0, slice(0, J))
         for jt in range(JT):
             second_layer(jt)

@@ -20,15 +20,35 @@ ACT = mybir.ActivationFunctionType
 P = 128
 PACK = 4
 BANK = 512
-JT = J // P
-RH = R // BANK
-UNITS = JT * RH
+POINT_TILES = J // P
+HALVES = R // BANK
+PIECES = HALVES * POINT_TILES
 LIST_COLS = J // 16
 
+ADDED_ON_VECTOR = (3, 7)
+SCALAR_BANKS, VECTOR_BANKS = 3, 5
 
-def load_scale_rows(queue, plane, rows):
-    for q in range(4):
-        queue.dma_start(out=plane[32 * q : 32 * q + 4, :], in_=rows[4 * q : 4 * q + 4, :].bitcast(I32))
+PIECE_STRIDE, NEIGHBOUR_STRIDE = 3, 4
+FIRST_LEAD = 2
+OWN_LAG = 3
+ADD_LAG = 3
+TURN_LAG = 6
+TURN_LAG_AFTER_ADD = 8
+ROUND_SECOND_HALF_AT = (3, 7)
+QUANTISE_SECOND_HALF_AT = 14
+RESULT_ON_VECTOR = 2
+
+
+def load_plane(nc, plane, rows):
+    for quadrant in range(4):
+        nc.sync.dma_start(
+            out=plane[32 * quadrant : 32 * quadrant + 4, :],
+            in_=rows[4 * quadrant : 4 * quadrant + 4, :].bitcast(I32),
+        )
+
+
+def load_words(nc, tile, words):
+    nc.sync.dma_start(out=tile[:].bitcast(I32), in_=words.bitcast(I32))
 
 
 def tile_list_pnet_mix_none_kernel(
@@ -37,240 +57,230 @@ def tile_list_pnet_mix_none_kernel(
     nc = tc.nc
     with ExitStack() as ctx:
         keep = ctx.enter_context(tc.tile_pool(name="keep", bufs=1))
-        ring = ctx.enter_context(tc.tile_pool(name="ring", bufs=4))
-        ps_s = ctx.enter_context(tc.psum_pool(name="ps_s", bufs=2))
-        ps_t = ctx.enter_context(tc.psum_pool(name="ps_t", bufs=1))
-        ps_v = ctx.enter_context(tc.psum_pool(name="ps_v", bufs=5))
+        psum = ctx.enter_context(tc.psum_pool(name="psum", bufs=1))
+
+        banks = [psum.tile([P, BANK], F32, name=f"bank{b}") for b in range(SCALAR_BANKS + VECTOR_BANKS)]
+        bank_sets = {"scalar": banks[:SCALAR_BANKS], "vector": banks[SCALAR_BANKS:]}
+        taken = {"scalar": [], "vector": []}
+
+        def next_bank(reader):
+            bank = bank_sets[reader][len(taken[reader]) % len(bank_sets[reader])]
+            taken[reader].append(bank)
+            return bank
 
         offsets = keep.tile([P, G * LIST_COLS], U16, name="offsets")
-        tab_sc = keep.tile([P, T // 4], I32, name="tab_sc", align_bytes=64)
-        w_sc = keep.tile([P, R // 4], I32, name="w_sc", align_bytes=64)
-        wd8_sc = keep.tile([P, N // 4], I32, name="wd8_sc", align_bytes=64)
-        wd4_sc = keep.tile([P, N // 4], I32, name="wd4_sc", align_bytes=64)
+        tab_plane = keep.tile([P, T // 4], I32, name="tab_plane", align_bytes=64)
+        w_plane = keep.tile([P, R // 4], I32, name="w_plane", align_bytes=64)
+        wd8_plane = keep.tile([P, N // 4], I32, name="wd8_plane", align_bytes=64)
+        wd4_plane = keep.tile([P, N // 4], I32, name="wd4_plane", align_bytes=64)
         tab_w = keep.tile([P, T], U32, name="tab_w", align_bytes=64)
         w_w = keep.tile([P, R], U32, name="w_w", align_bytes=64)
         wd8_w = keep.tile([P, N], U32, name="wd8_w", align_bytes=64)
         wd4_w = keep.tile([P, 2 * N], U8, name="wd4_w", align_bytes=64)
+        c_raw = keep.tile([P, PACK, J], F32, name="c_raw")
+        wc_raw = [keep.tile([P, PACK, BANK], F32, name=f"wc_raw{h}") for h in range(HALVES)]
         ident = keep.tile([P, P], F32, name="ident")
 
-        nc.vector.memset(tab_sc[:, : T // 8], 0)
-        nc.gpsimd.memset(tab_sc[:, T // 8 :], 0)
-        nc.vector.memset(w_sc[:], 0)
-        nc.vector.memset(wd8_sc[:], 0)
-        nc.vector.memset(wd4_sc[:], 0)
+        nc.vector.memset(tab_plane[:, : T // 8], 0)
+        nc.gpsimd.memset(tab_plane[:, T // 8 :], 0)
+        nc.vector.memset(w_plane[:], 0)
+        nc.vector.memset(wd8_plane[:], 0)
+        nc.vector.memset(wd4_plane[:], 0)
         make_identity(nc, ident[:])
-        c_raw = keep.tile([P, PACK, J], F32, name="c_raw", tag="stage_c")
-        wc_raw = [keep.tile([P, PACK, BANK], F32, name=f"wc_raw{h}", tag=f"stage_wc{h}") for h in range(RH)]
 
+        wc_rows = wc.rearrange("(p i) r -> p i r", i=PACK)
+        parts = (slice(0, BANK // 2), slice(BANK // 2, BANK))
         nc.sync.dma_start(offsets[:], offs)
-        load_scale_rows(nc.sync, tab_sc, tab_scales[0])
-        nc.sync.dma_start(out=wd4_w[:].bitcast(I32), in_=wd4_words[0].bitcast(I32))
+        load_plane(nc, tab_plane, tab_scales[0])
+        load_words(nc, tab_w, tab_words[0].rearrange("p t i -> p (t i)"))
+        for part in parts:
+            nc.sync.dma_start(out=wc_raw[0][:, :, part], in_=wc_rows[:, :, part])
         nc.sync.dma_start(out=c_raw[:], in_=c.rearrange("(p i) j -> p i j", i=PACK))
-        nc.sync.dma_start(out=tab_w[:].bitcast(I32), in_=tab_words[0].rearrange("p t i -> p (t i)").bitcast(I32))
-        nc.sync.dma_start(out=w_w[:].bitcast(I32), in_=w_words[0].rearrange("p r i -> p (r i)").bitcast(I32))
-        load_scale_rows(nc.sync, w_sc, w_scales[0])
-        for h in range(RH):
-            nc.sync.dma_start(
-                out=wc_raw[h][:], in_=wc[:, h * BANK : (h + 1) * BANK].rearrange("(p i) r -> p i r", i=PACK)
-            )
-        load_scale_rows(nc.sync, wd8_sc, wd8_scales[0])
-        load_scale_rows(nc.sync, wd4_sc, wd4_scales[0])
-        nc.sync.dma_start(out=wd8_w[:].bitcast(I32), in_=wd8_words[0].rearrange("p n i -> p (n i)").bitcast(I32))
+        load_plane(nc, w_plane, w_scales[0])
+        load_words(nc, w_w, w_words[0].rearrange("p r i -> p (r i)"))
+        nc.sync.dma_start(out=wc_raw[1][:], in_=wc_rows[:, :, BANK:])
+        load_words(nc, wd4_w, wd4_words[0])
+        load_words(nc, wd8_w, wd8_words[0].rearrange("p n i -> p (n i)"))
+        load_plane(nc, wd4_plane, wd4_scales[0])
+        load_plane(nc, wd8_plane, wd8_scales[0])
 
         nb_w = [keep.tile([P, J], U32, name=f"nb_w{g}", align_bytes=64) for g in range(G)]
-        nb_sc = [keep.tile([P, 2 * J], U8, name=f"nb_sc{g2}", align_bytes=64) for g2 in range(G // 2)]
-        for g2 in range(G // 2):
-            nc.vector.tensor_copy(
-                nb_sc[g2][:],
-                tab_sc[:].bitcast(U8).indirect(offsets[:, 2 * g2 * LIST_COLS : 2 * (g2 + 1) * LIST_COLS]),
-            )
-            for g in (2 * g2, 2 * g2 + 1):
-                nc.vector.tensor_copy(
-                    nb_w[g][:], tab_w[:].indirect(offsets[:, g * LIST_COLS : (g + 1) * LIST_COLS])
-                )
+        nb_plane = [keep.tile([P, 2 * J], U8, name=f"nb_plane{pair}", align_bytes=64) for pair in range(G // 2)]
+        for pair in range(G // 2):
+            entries = offsets[:, 2 * pair * LIST_COLS : 2 * (pair + 1) * LIST_COLS]
+            nc.vector.tensor_copy(nb_plane[pair][:], tab_plane[:].bitcast(U8).indirect(entries))
+        for g in range(G):
+            nc.vector.tensor_copy(nb_w[g][:], tab_w[:].indirect(offsets[:, g * LIST_COLS : (g + 1) * LIST_COLS]))
 
         c_w = keep.tile([P, J], U32, name="c_w", align_bytes=64)
-        c_sc = keep.tile([P, J], U8, name="c_sc", align_bytes=64)
-        wc_w = [keep.tile([P, BANK], U32, name=f"wc_w{h}", align_bytes=64) for h in range(RH)]
-        wc_sc = [keep.tile([P, BANK], U8, name=f"wc_sc{h}", align_bytes=64) for h in range(RH)]
+        c_plane = keep.tile([P, J], U8, name="c_plane", align_bytes=64)
+        wc_w = [keep.tile([P, BANK], U32, name=f"wc_w{h}", align_bytes=64) for h in range(HALVES)]
+        wc_plane = [keep.tile([P, BANK], U8, name=f"wc_plane{h}", align_bytes=64) for h in range(HALVES)]
+        wc_bf = [keep.tile([P, BANK, PACK], BF16, name=f"wc_bf{h}", align_bytes=64) for h in range(HALVES)]
+        c_bf = keep.tile([P, J, PACK], BF16, name="c_bf", align_bytes=64)
 
-        def quantise(raw, words, scales, name, on_gpsimd):
-            grouped = keep.tile([P, BANK, PACK], BF16, name=name, align_bytes=64)
-            if on_gpsimd:
-                for s in range(4):
-                    cols = slice(s * P, (s + 1) * P)
-                    nc.gpsimd.tensor_scalar(
-                        grouped[:, cols, :],
-                        raw[:, :, cols].rearrange("p i a -> p a i"),
-                        1.0,
-                        0.0,
-                        ALU.mult,
-                        ALU.add,
-                    )
-            else:
-                nc.scalar.activation(
-                    grouped[:].rearrange("p (a b) i -> p a i b", b=4),
-                    raw[:].rearrange("p i (a b) -> p a i b", b=4),
-                    ACT.Copy,
-                )
+        def round_rows(rounded, raw, cols):
+            nc.scalar.activation(
+                rounded[:, cols, :].rearrange("p (a b) i -> p a i b", b=4),
+                raw[:, :, cols].rearrange("p i (a b) -> p a i b", b=4),
+                ACT.Copy,
+            )
+
+        def quantise(words, plane, rounded, cols):
             nc.vector.quantize_mx(
-                out=words[:].bitcast(FP8X4), scales=scales[:], in_=grouped[:].rearrange("p a i -> p (a i)")
+                out=words[:, cols].bitcast(FP8X4),
+                scales=plane[:, cols],
+                in_=rounded[:, cols, :].rearrange("p a i -> p (a i)"),
             )
 
-        def nb_pass(bank, u, g, start, stop):
-            h, jt = divmod(u, JT)
-            nc.tensor.matmul_mx(
-                out=bank[:],
-                lhsT=nb_w[g][:, jt * P : (jt + 1) * P].bitcast(FP8X4),
-                lhsT_scale=nb_sc[g // 2][:, (g % 2) * J + jt * P : (g % 2) * J + (jt + 1) * P],
-                rhs=w_w[:, h * BANK : (h + 1) * BANK].bitcast(FP8X4),
-                rhs_scale=w_sc[:].bitcast(U8)[:, h * BANK : (h + 1) * BANK],
-                start=start,
-                stop=stop,
-            )
-
-        def own_pass(bank, u, start, stop):
-            h, jt = divmod(u, JT)
-            nc.tensor.matmul_mx(
-                out=bank[:],
-                lhsT=c_w[:, jt * P : (jt + 1) * P].bitcast(FP8X4),
-                lhsT_scale=c_sc[:, jt * P : (jt + 1) * P],
-                rhs=wc_w[h][:].bitcast(FP8X4),
-                rhs_scale=wc_sc[h][:],
-                start=start,
-                stop=stop,
-            )
-
-        ON_VECTOR = (6, 7)
-
-        def by_slot(bank, u):
-            if u in ON_VECTOR:
+        def from_bank(bank, u):
+            if u in ADDED_ON_VECTOR:
                 return bank[:].rearrange("j (p a e) -> j a p e", a=2, e=2)
             return bank[:].rearrange("j (p t) -> j t p", t=PACK)
 
-        def like_slot(flat, u):
-            if u in ON_VECTOR:
-                return flat.rearrange("j (a p e) -> j a p e", a=2, e=2)
-            return flat.rearrange("j (t p) -> j t p", t=PACK)
+        def in_sbuf(tile, u):
+            if u in ADDED_ON_VECTOR:
+                return tile[:].rearrange("j (a p e) -> j a p e", a=2, e=2)
+            return tile[:].rearrange("j (t p) -> j t p", t=PACK)
 
-        pooled = {}
-
-        def claim(units, tag):
-            shared = keep.tile([P, len(units), BANK], F32, name=f"pooled_{tag}", tag=tag)
-            for i, u in enumerate(units):
-                pooled[u] = shared[:, i, :]
-
+        pooled = [keep.tile([P, BANK], F32, name=f"pooled{u}") for u in range(PIECES)]
+        h_bf = [keep.tile([P, J, PACK], BF16, name=f"h_bf{h}", align_bytes=64) for h in range(HALVES)]
+        h_w = [keep.tile([P, J], U32, name=f"h_w{h}", align_bytes=64) for h in range(HALVES)]
+        h_plane = [keep.tile([P, J], U8, name=f"h_plane{h}", align_bytes=64) for h in range(HALVES)]
+        own = {u: keep.tile([P, BANK], F32, name=f"own{u}") for u in range(PIECES) if u not in ADDED_ON_VECTOR}
         summed = {}
-        h_bf = [keep.tile([P, J, PACK], BF16, name=f"h_bf{h}", align_bytes=64) for h in range(RH)]
-        h_w = [keep.tile([P, J], U32, name=f"h_w{h}", align_bytes=64) for h in range(RH)]
-        h_sc = [keep.tile([P, J], U8, name=f"h_sc{h}", align_bytes=64) for h in range(RH)]
 
         def neighbour(u, g):
-            bank = (ps_s if g == 0 else ps_v).tile([P, BANK], F32, name="bank", tag="bank")
-            nb_pass(bank, u, g, True, True)
+            h, jt = divmod(u, POINT_TILES)
+            first = (g % 2) * J + jt * P
+            bank = next_bank("scalar" if g == 0 else "vector")
+            nc.tensor.matmul_mx(
+                out=bank[:],
+                lhsT=nb_w[g][:, jt * P : (jt + 1) * P].bitcast(FP8X4),
+                lhsT_scale=nb_plane[g // 2][:, first : first + P],
+                rhs=w_w[:, h * BANK : (h + 1) * BANK].bitcast(FP8X4),
+                rhs_scale=w_plane[:].bitcast(U8)[:, h * BANK : (h + 1) * BANK],
+                start=True,
+                stop=True,
+            )
             if g == 0:
-                nc.scalar.activation(like_slot(pooled[u], u), by_slot(bank, u), ACT.Copy)
+                nc.scalar.activation(in_sbuf(pooled[u], u), from_bank(bank, u), ACT.Copy)
             else:
-                nc.vector.tensor_tensor(like_slot(pooled[u], u), by_slot(bank, u), like_slot(pooled[u], u), ALU.max)
-
-        own = {u: keep.tile([P, BANK], F32, name=f"own{u}") for u in range(UNITS) if u not in ON_VECTOR}
+                nc.vector.tensor_tensor(in_sbuf(pooled[u], u), from_bank(bank, u), in_sbuf(pooled[u], u), ALU.max)
 
         def own_part(u):
-            bank = (ps_v if u in ON_VECTOR else ps_s).tile([P, BANK], F32, name="bank", tag="bank")
-            own_pass(bank, u, True, True)
-            if u in ON_VECTOR:
-                summed[u] = ring.tile([P, BANK], BF16, name="summed")
-                nc.vector.tensor_tensor(like_slot(summed[u][:], u), by_slot(bank, u), like_slot(pooled[u], u), ALU.add)
+            h, jt = divmod(u, POINT_TILES)
+            bank = next_bank("vector" if u in ADDED_ON_VECTOR else "scalar")
+            nc.tensor.matmul_mx(
+                out=bank[:],
+                lhsT=c_w[:, jt * P : (jt + 1) * P].bitcast(FP8X4),
+                lhsT_scale=c_plane[:, jt * P : (jt + 1) * P],
+                rhs=wc_w[h][:].bitcast(FP8X4),
+                rhs_scale=wc_plane[h][:],
+                start=True,
+                stop=True,
+            )
+            if u in ADDED_ON_VECTOR:
+                summed[u] = keep.tile([P, BANK], BF16, name=f"summed{u}")
+                nc.vector.tensor_tensor(in_sbuf(summed[u], u), from_bank(bank, u), in_sbuf(pooled[u], u), ALU.add)
             else:
-                nc.scalar.activation(like_slot(own[u][:], u), by_slot(bank, u), ACT.Copy)
+                nc.scalar.activation(in_sbuf(own[u], u), from_bank(bank, u), ACT.Copy)
 
-        def finish(u):
-            h, jt = divmod(u, JT)
-            dst = h_bf[h][:, jt * P : (jt + 1) * P, :]
-            if u in ON_VECTOR:
-                turned = ps_s.tile([P, 2, P], F32, name="turned", tag="bank")
-                words = summed[u][:].bitcast(F32)
+        def turn(u):
+            h, jt = divmod(u, POINT_TILES)
+            rounded = h_bf[h][:, jt * P : (jt + 1) * P, :]
+            if u in ADDED_ON_VECTOR:
+                turned = next_bank("scalar")[:, : 2 * P].rearrange("p (a j) -> p a j", a=2)
+                pairs = summed[u][:].bitcast(F32)
                 for a in range(2):
-                    nc.tensor.transpose(turned[:, a, :], words[:, a * P : (a + 1) * P], ident[:])
+                    nc.tensor.transpose(turned[:, a, :], pairs[:, a * P : (a + 1) * P], ident[:])
                 nc.scalar.activation(
-                    dst.rearrange("p j (a e) -> p j a e", e=2),
-                    turned[:].bitcast(BF16).rearrange("p a (j e) -> p j a e", e=2),
+                    rounded.rearrange("p j (a e) -> p j a e", e=2),
+                    turned.bitcast(BF16).rearrange("p a (j e) -> p j a e", e=2),
                     ACT.Relu,
                 )
             else:
-                turned = ps_t.tile([P, PACK, P], F32, name="turned")
+                turned = next_bank("scalar")[:].rearrange("p (t j) -> p t j", t=PACK)
                 for t in range(PACK):
                     cols = slice(t * P, (t + 1) * P)
-                    nc.tensor.matmul(turned[:, t, :], own[u][:, cols], ident[:], start=True, stop=False, is_transpose=True)
-                    nc.tensor.matmul(turned[:, t, :], pooled[u][:, cols], ident[:], start=False, stop=True, is_transpose=True)
-                nc.scalar.activation(dst, turned[:].rearrange("p t j -> p j t"), ACT.Relu)
+                    for term, start in ((own[u], True), (pooled[u], False)):
+                        nc.tensor.matmul(
+                            turned[:, t, :], term[:, cols], ident[:], start=start, stop=not start, is_transpose=True
+                        )
+                nc.scalar.activation(rounded, turned.rearrange("p t j -> p j t"), ACT.Relu)
 
-        def quantise_h(h, points):
-            nc.vector.quantize_mx(
-                out=h_w[h][:, points].bitcast(FP8X4),
-                scales=h_sc[h][:, points],
-                in_=h_bf[h][:, points, :].rearrange("p j t -> p (j t)"),
+        def result_passes(y, nt, points):
+            nc.tensor.matmul_mx(
+                out=y,
+                lhsT=wd8_w[:, nt * P : (nt + 1) * P].bitcast(FP8X4),
+                lhsT_scale=wd8_plane[:].bitcast(U8)[:, nt * P : (nt + 1) * P],
+                rhs=h_w[0][:, points].bitcast(FP8X4),
+                rhs_scale=h_plane[0][:, points],
+                start=True,
+                stop=False,
+            )
+            nc.tensor.matmul_mx(
+                out=y,
+                lhsT=wd4_w[:, 2 * nt * P : 2 * (nt + 1) * P].bitcast(FP4X4),
+                lhsT_scale=wd4_plane[:].bitcast(U8)[:, nt * P : (nt + 1) * P],
+                rhs=h_w[1][:, points].bitcast(FP8X4),
+                rhs_scale=h_plane[1][:, points],
+                start=False,
+                stop=True,
             )
 
         def second_layer(jt):
             points = slice(jt * P, (jt + 1) * P)
-            quantise_h(1, points)
-            y = ps_v.tile([P, N // P, P], F32, name="y", tag="bank")
-            for nt in range(N // P):
-                nc.tensor.matmul_mx(
-                    out=y[:, nt, :],
-                    lhsT=wd8_w[:, nt * P : (nt + 1) * P].bitcast(FP8X4),
-                    lhsT_scale=wd8_sc[:].bitcast(U8)[:, nt * P : (nt + 1) * P],
-                    rhs=h_w[0][:, points].bitcast(FP8X4),
-                    rhs_scale=h_sc[0][:, points],
-                    start=True,
-                    stop=False,
-                )
-                nc.tensor.matmul_mx(
-                    out=y[:, nt, :],
-                    lhsT=wd4_w[:, 2 * nt * P : 2 * (nt + 1) * P].bitcast(FP4X4),
-                    lhsT_scale=wd4_sc[:].bitcast(U8)[:, nt * P : (nt + 1) * P],
-                    rhs=h_w[1][:, points].bitcast(FP8X4),
-                    rhs_scale=h_sc[1][:, points],
-                    start=False,
-                    stop=True,
-                )
-            y_sb = ring.tile([P, N // P, P], F32, name="y_sb")
-            if jt % 2 == 0:
-                nc.vector.tensor_copy(y_sb[:], y[:])
+            quantise(h_w[1], h_plane[1], h_bf[1], points)
+            y_sb = keep.tile([P, N // P, P], F32, name=f"y_sb{jt}")
+            if jt == POINT_TILES - 1:
+                upper = next_bank("vector")[:, :P]
+                result_passes(upper, 0, points)
+                nc.vector.tensor_copy(y_sb[:, 0, :], upper)
+                nc.sync.dma_start(out=out[:P, points], in_=y_sb[:, 0, :])
+                lower = next_bank("vector")[:, :P]
+                result_passes(lower, 1, points)
+                nc.scalar.activation(y_sb[:, 1, :], lower, ACT.Copy)
+                nc.scalar.dma_start(out=out[P:, points], in_=y_sb[:, 1, :])
             else:
-                nc.scalar.activation(y_sb[:], y[:], ACT.Copy)
-            nc.sync.dma_start(
-                out=out[:, jt * P : (jt + 1) * P].rearrange("(nt n) j -> n nt j", n=P), in_=y_sb[:]
-            )
+                y = next_bank("vector")[:, :N].rearrange("n (nt j) -> n nt j", j=P)
+                for nt in range(N // P):
+                    result_passes(y[:, nt, :], nt, points)
+                if jt == RESULT_ON_VECTOR:
+                    nc.vector.tensor_copy(y_sb[:], y)
+                else:
+                    nc.scalar.activation(y_sb[:], y, ACT.Copy)
+                nc.sync.dma_start(out=out[:, points].rearrange("(nt n) j -> n nt j", n=P), in_=y_sb[:])
 
-        EARLY = 4
-        quantise(c_raw, c_w, c_sc, "c_bf", False)
-        claim([0, 1], "stage_c")
-        neighbour(0, 0)
-        neighbour(1, 0)
-        quantise(wc_raw[0], wc_w[0], wc_sc[0], "wc_bf0", False)
-        claim([2, 3], "stage_wc0")
-        neighbour(2, 0)
-        neighbour(3, 0)
-        quantise(wc_raw[1], wc_w[1], wc_sc[1], "wc_bf1", False)
-        claim([4, 5, 6, 7], "stage_wc1")
-        for u in range(UNITS + 1):
-            if u < UNITS and u not in ON_VECTOR:
-                own_part(u)
-            if u + EARLY < UNITS:
-                neighbour(u + EARLY, 0)
-            if u < UNITS:
-                neighbour(u, 1)
-            if u >= 1:
-                neighbour(u - 1, 3)
-            if u < UNITS:
-                neighbour(u, 2)
-            if u - 1 in ON_VECTOR:
-                own_part(u - 1)
-            if u >= 2:
-                finish(u - 2)
-        finish(UNITS - 1)
-        quantise_h(0, slice(0, J))
-        for jt in range(JT):
+        whole = slice(0, BANK)
+        for part in parts:
+            round_rows(wc_bf[0], wc_raw[0], part)
+        quantise(wc_w[0], wc_plane[0], wc_bf[0], whole)
+        round_rows(c_bf, c_raw, whole)
+        quantise(c_w, c_plane, c_bf, whole)
+
+        maxima = sorted(
+            ((u, g) for u in range(PIECES) for g in range(1, G)),
+            key=lambda ug: (PIECE_STRIDE * ug[0] + NEIGHBOUR_STRIDE * ug[1], ug[0]),
+        )
+        last = {u: place for place, (u, g) in enumerate(maxima)}
+        steps = [
+            (place, round_rows, (wc_bf[1], wc_raw[1], part)) for place, part in zip(ROUND_SECOND_HALF_AT, parts)
+        ]
+        steps.append((QUANTISE_SECOND_HALF_AT, quantise, (wc_w[1], wc_plane[1], wc_bf[1], whole)))
+        steps.extend((u - FIRST_LEAD, neighbour, (u, 0)) for u in range(PIECES))
+        steps.extend(
+            (last[u] + ADD_LAG if u in ADDED_ON_VECTOR else PIECE_STRIDE * u + OWN_LAG, own_part, (u,))
+            for u in range(PIECES)
+        )
+        steps.extend(
+            (last[u] + (TURN_LAG_AFTER_ADD if u in ADDED_ON_VECTOR else TURN_LAG), turn, (u,)) for u in range(PIECES)
+        )
+        steps.extend((place, neighbour, ug) for place, ug in enumerate(maxima))
+        for place, call, arguments in sorted(steps, key=lambda step: step[0]):
+            call(*arguments)
+
+        for points in (slice(0, J // 2), slice(J // 2, J)):
+            quantise(h_w[0], h_plane[0], h_bf[0], points)
+        for jt in range(POINT_TILES):
             second_layer(jt)

@@ -25,18 +25,21 @@ HALVES = R // BANK
 PIECES = HALVES * POINT_TILES
 LIST_COLS = J // 16
 
-ADDED_ON_VECTOR = (3, 7)
-SCALAR_BANKS, VECTOR_BANKS = 3, 5
+ADDED_ON_VECTOR = 7
+ADDED_IN_EACH_SUM = 3
+ROUNDED_EARLY = (ADDED_ON_VECTOR, ADDED_IN_EACH_SUM)
+SCALAR_BANKS, VECTOR_BANKS = 4, 4
 
-PIECE_STRIDE, NEIGHBOUR_STRIDE = 3, 4
-FIRST_LEAD = 2
-OWN_LAG = 3
-ADD_LAG = 3
+PIECE_STRIDE, NEIGHBOUR_STRIDE = 3, 5
+FIRST_LEAD = 8
+OWN_LAG = 6
 TURN_LAG = 6
-TURN_LAG_AFTER_ADD = 8
-ROUND_SECOND_HALF_AT = (3, 7)
-QUANTISE_SECOND_HALF_AT = 14
-RESULT_ON_VECTOR = 2
+ROUND_SECOND_HALF_AT = (2, 5)
+QUANTISE_SECOND_HALF_AT = 10
+EACH_SUM_AT = (5, 7, 9, 11)
+FOLD_AT = (17, 19)
+FOLDED_TURN_AT = 21
+SPLIT_RESULTS = (2, 3)
 
 
 def load_plane(nc, plane, rows):
@@ -89,28 +92,27 @@ def tile_list_pnet_mix_none_kernel(
         make_identity(nc, ident[:])
 
         wc_rows = wc.rearrange("(p i) r -> p i r", i=PACK)
-        parts = (slice(0, BANK // 2), slice(BANK // 2, BANK))
         nc.sync.dma_start(offsets[:], offs)
         load_plane(nc, tab_plane, tab_scales[0])
         load_words(nc, tab_w, tab_words[0].rearrange("p t i -> p (t i)"))
-        for part in parts:
-            nc.sync.dma_start(out=wc_raw[0][:, :, part], in_=wc_rows[:, :, part])
         nc.sync.dma_start(out=c_raw[:], in_=c.rearrange("(p i) j -> p i j", i=PACK))
-        load_plane(nc, w_plane, w_scales[0])
+        nc.sync.dma_start(out=wc_raw[0][:], in_=wc_rows[:, :, :BANK])
         load_words(nc, w_w, w_words[0].rearrange("p r i -> p (r i)"))
+        load_plane(nc, w_plane, w_scales[0])
         nc.sync.dma_start(out=wc_raw[1][:], in_=wc_rows[:, :, BANK:])
         load_words(nc, wd4_w, wd4_words[0])
         load_words(nc, wd8_w, wd8_words[0].rearrange("p n i -> p (n i)"))
         load_plane(nc, wd4_plane, wd4_scales[0])
         load_plane(nc, wd8_plane, wd8_scales[0])
 
-        nb_w = [keep.tile([P, J], U32, name=f"nb_w{g}", align_bytes=64) for g in range(G)]
+        nb_w = keep.tile([P, G, J], U32, name="nb_w", align_bytes=64)
         nb_plane = [keep.tile([P, 2 * J], U8, name=f"nb_plane{pair}", align_bytes=64) for pair in range(G // 2)]
+        entries = [offsets[:, 2 * pair * LIST_COLS : 2 * (pair + 1) * LIST_COLS] for pair in range(G // 2)]
         for pair in range(G // 2):
-            entries = offsets[:, 2 * pair * LIST_COLS : 2 * (pair + 1) * LIST_COLS]
-            nc.vector.tensor_copy(nb_plane[pair][:], tab_plane[:].bitcast(U8).indirect(entries))
-        for g in range(G):
-            nc.vector.tensor_copy(nb_w[g][:], tab_w[:].indirect(offsets[:, g * LIST_COLS : (g + 1) * LIST_COLS]))
+            nc.vector.tensor_copy(nb_plane[pair][:], tab_plane[:].bitcast(U8).indirect(entries[pair]))
+        for pair in range(G // 2):
+            picked = nb_w[:, 2 * pair : 2 * (pair + 1), :].rearrange("p g j -> p (g j)")
+            nc.vector.tensor_copy(picked, tab_w[:].indirect(entries[pair]))
 
         c_w = keep.tile([P, J], U32, name="c_w", align_bytes=64)
         c_plane = keep.tile([P, J], U8, name="c_plane", align_bytes=64)
@@ -134,43 +136,40 @@ def tile_list_pnet_mix_none_kernel(
             )
 
         def from_bank(bank, u):
-            if u in ADDED_ON_VECTOR:
+            if u in ROUNDED_EARLY:
                 return bank[:].rearrange("j (p a e) -> j a p e", a=2, e=2)
             return bank[:].rearrange("j (p t) -> j t p", t=PACK)
 
-        def in_sbuf(tile, u):
-            if u in ADDED_ON_VECTOR:
-                return tile[:].rearrange("j (a p e) -> j a p e", a=2, e=2)
-            return tile[:].rearrange("j (t p) -> j t p", t=PACK)
+        def in_sbuf(columns, u):
+            if u in ROUNDED_EARLY:
+                return columns.rearrange("j (a p e) -> j a p e", a=2, e=2)
+            return columns.rearrange("j (t p) -> j t p", t=PACK)
 
-        pooled = [keep.tile([P, BANK], F32, name=f"pooled{u}") for u in range(PIECES)]
+        ranked = [u for u in range(PIECES) if u != ADDED_IN_EACH_SUM]
+        pooled = {u: keep.tile([P, BANK], F32, name=f"pooled{u}") for u in ranked}
+        own = {u: keep.tile([P, BANK], F32, name=f"own{u}") for u in ranked if u != ADDED_ON_VECTOR}
+        summed = {u: keep.tile([P, BANK], BF16, name=f"summed{u}") for u in ROUNDED_EARLY}
+        four_sums = keep.tile([P, G, BANK], BF16, name="four_sums")
+        two_sums = keep.tile([P, G // 2, BANK], BF16, name="two_sums")
         h_bf = [keep.tile([P, J, PACK], BF16, name=f"h_bf{h}", align_bytes=64) for h in range(HALVES)]
         h_w = [keep.tile([P, J], U32, name=f"h_w{h}", align_bytes=64) for h in range(HALVES)]
         h_plane = [keep.tile([P, J], U8, name=f"h_plane{h}", align_bytes=64) for h in range(HALVES)]
-        own = {u: keep.tile([P, BANK], F32, name=f"own{u}") for u in range(PIECES) if u not in ADDED_ON_VECTOR}
-        summed = {}
 
-        def neighbour(u, g):
+        def neighbour_pass(bank, u, g, start):
             h, jt = divmod(u, POINT_TILES)
             first = (g % 2) * J + jt * P
-            bank = next_bank("scalar" if g == 0 else "vector")
             nc.tensor.matmul_mx(
                 out=bank[:],
-                lhsT=nb_w[g][:, jt * P : (jt + 1) * P].bitcast(FP8X4),
+                lhsT=nb_w[:, g, jt * P : (jt + 1) * P].bitcast(FP8X4),
                 lhsT_scale=nb_plane[g // 2][:, first : first + P],
                 rhs=w_w[:, h * BANK : (h + 1) * BANK].bitcast(FP8X4),
                 rhs_scale=w_plane[:].bitcast(U8)[:, h * BANK : (h + 1) * BANK],
-                start=True,
+                start=start,
                 stop=True,
             )
-            if g == 0:
-                nc.scalar.activation(in_sbuf(pooled[u], u), from_bank(bank, u), ACT.Copy)
-            else:
-                nc.vector.tensor_tensor(in_sbuf(pooled[u], u), from_bank(bank, u), in_sbuf(pooled[u], u), ALU.max)
 
-        def own_part(u):
+        def own_pass(bank, u, stop):
             h, jt = divmod(u, POINT_TILES)
-            bank = next_bank("vector" if u in ADDED_ON_VECTOR else "scalar")
             nc.tensor.matmul_mx(
                 out=bank[:],
                 lhsT=c_w[:, jt * P : (jt + 1) * P].bitcast(FP8X4),
@@ -178,27 +177,54 @@ def tile_list_pnet_mix_none_kernel(
                 rhs=wc_w[h][:].bitcast(FP8X4),
                 rhs_scale=wc_plane[h][:],
                 start=True,
-                stop=True,
+                stop=stop,
             )
-            if u in ADDED_ON_VECTOR:
-                summed[u] = keep.tile([P, BANK], BF16, name=f"summed{u}")
-                nc.vector.tensor_tensor(in_sbuf(summed[u], u), from_bank(bank, u), in_sbuf(pooled[u], u), ALU.add)
+
+        def neighbour(u, g):
+            bank = next_bank("scalar" if g == 0 else "vector")
+            neighbour_pass(bank, u, g, True)
+            running = in_sbuf(pooled[u][:], u)
+            if g == 0:
+                nc.scalar.activation(running, from_bank(bank, u), ACT.Copy)
             else:
-                nc.scalar.activation(in_sbuf(own[u], u), from_bank(bank, u), ACT.Copy)
+                nc.vector.tensor_tensor(running, from_bank(bank, u), running, ALU.max)
+
+        def own_part(u):
+            bank = next_bank("vector" if u == ADDED_ON_VECTOR else "scalar")
+            own_pass(bank, u, True)
+            if u == ADDED_ON_VECTOR:
+                nc.vector.tensor_tensor(in_sbuf(summed[u][:], u), from_bank(bank, u), in_sbuf(pooled[u][:], u), ALU.add)
+            else:
+                nc.scalar.activation(in_sbuf(own[u][:], u), from_bank(bank, u), ACT.Copy)
+
+        def neighbour_with_own_part(g):
+            bank = next_bank("scalar")
+            own_pass(bank, ADDED_IN_EACH_SUM, False)
+            neighbour_pass(bank, ADDED_IN_EACH_SUM, g, False)
+            nc.scalar.activation(
+                in_sbuf(four_sums[:, g, :], ADDED_IN_EACH_SUM), from_bank(bank, ADDED_IN_EACH_SUM), ACT.Relu
+            )
+
+        def fold(result, lower, upper):
+            nc.vector.tensor_tensor(result, lower, upper, ALU.max)
 
         def turn(u):
             h, jt = divmod(u, POINT_TILES)
             rounded = h_bf[h][:, jt * P : (jt + 1) * P, :]
-            if u in ADDED_ON_VECTOR:
+            if u in ROUNDED_EARLY:
                 turned = next_bank("scalar")[:, : 2 * P].rearrange("p (a j) -> p a j", a=2)
                 pairs = summed[u][:].bitcast(F32)
                 for a in range(2):
                     nc.tensor.transpose(turned[:, a, :], pairs[:, a * P : (a + 1) * P], ident[:])
-                nc.scalar.activation(
-                    rounded.rearrange("p j (a e) -> p j a e", e=2),
-                    turned.bitcast(BF16).rearrange("p a (j e) -> p j a e", e=2),
-                    ACT.Relu,
-                )
+                if u == ADDED_IN_EACH_SUM:
+                    rounded_pairs = rounded.rearrange("p j t -> p (j t)").bitcast(F32)
+                    nc.scalar.copy(rounded_pairs.rearrange("p (j a) -> p j a", a=2), turned.rearrange("p a j -> p j a"))
+                else:
+                    nc.scalar.activation(
+                        rounded.rearrange("p j (a e) -> p j a e", e=2),
+                        turned.bitcast(BF16).rearrange("p a (j e) -> p j a e", e=2),
+                        ACT.Relu,
+                    )
             else:
                 turned = next_bank("scalar")[:].rearrange("p (t j) -> p t j", t=PACK)
                 for t in range(PACK):
@@ -233,7 +259,7 @@ def tile_list_pnet_mix_none_kernel(
             points = slice(jt * P, (jt + 1) * P)
             quantise(h_w[1], h_plane[1], h_bf[1], points)
             y_sb = keep.tile([P, N // P, P], F32, name=f"y_sb{jt}")
-            if jt == POINT_TILES - 1:
+            if jt in SPLIT_RESULTS:
                 upper = next_bank("vector")[:, :P]
                 result_passes(upper, 0, points)
                 nc.vector.tensor_copy(y_sb[:, 0, :], upper)
@@ -246,36 +272,38 @@ def tile_list_pnet_mix_none_kernel(
                 y = next_bank("vector")[:, :N].rearrange("n (nt j) -> n nt j", j=P)
                 for nt in range(N // P):
                     result_passes(y[:, nt, :], nt, points)
-                if jt == RESULT_ON_VECTOR:
-                    nc.vector.tensor_copy(y_sb[:], y)
-                else:
-                    nc.scalar.activation(y_sb[:], y, ACT.Copy)
+                nc.scalar.activation(y_sb[:], y, ACT.Copy)
                 nc.sync.dma_start(out=out[:, points].rearrange("(nt n) j -> n nt j", n=P), in_=y_sb[:])
 
         whole = slice(0, BANK)
-        for part in parts:
-            round_rows(wc_bf[0], wc_raw[0], part)
-        quantise(wc_w[0], wc_plane[0], wc_bf[0], whole)
         round_rows(c_bf, c_raw, whole)
         quantise(c_w, c_plane, c_bf, whole)
+        round_rows(wc_bf[0], wc_raw[0], whole)
+        quantise(wc_w[0], wc_plane[0], wc_bf[0], whole)
 
         maxima = sorted(
-            ((u, g) for u in range(PIECES) for g in range(1, G)),
-            key=lambda ug: (PIECE_STRIDE * ug[0] + NEIGHBOUR_STRIDE * ug[1], ug[0]),
+            ((u, g) for u in ranked for g in range(1, G)),
+            key=lambda ug: (PIECE_STRIDE * ranked.index(ug[0]) + NEIGHBOUR_STRIDE * ug[1], ug[0]),
         )
         last = {u: place for place, (u, g) in enumerate(maxima)}
+        parts = (slice(0, BANK // 2), slice(BANK // 2, BANK))
+        folds = (
+            (two_sums[:], four_sums[:, :2, :], four_sums[:, 2:, :]),
+            (summed[ADDED_IN_EACH_SUM][:], two_sums[:, 0, :], two_sums[:, 1, :]),
+        )
         steps = [
             (place, round_rows, (wc_bf[1], wc_raw[1], part)) for place, part in zip(ROUND_SECOND_HALF_AT, parts)
         ]
         steps.append((QUANTISE_SECOND_HALF_AT, quantise, (wc_w[1], wc_plane[1], wc_bf[1], whole)))
-        steps.extend((u - FIRST_LEAD, neighbour, (u, 0)) for u in range(PIECES))
+        steps.extend((PIECE_STRIDE * rank - FIRST_LEAD, neighbour, (u, 0)) for rank, u in enumerate(ranked))
+        steps.extend((place, neighbour_with_own_part, (g,)) for g, place in enumerate(EACH_SUM_AT))
         steps.extend(
-            (last[u] + ADD_LAG if u in ADDED_ON_VECTOR else PIECE_STRIDE * u + OWN_LAG, own_part, (u,))
-            for u in range(PIECES)
+            (last[u] + 1 if u == ADDED_ON_VECTOR else PIECE_STRIDE * rank + OWN_LAG, own_part, (u,))
+            for rank, u in enumerate(ranked)
         )
-        steps.extend(
-            (last[u] + (TURN_LAG_AFTER_ADD if u in ADDED_ON_VECTOR else TURN_LAG), turn, (u,)) for u in range(PIECES)
-        )
+        steps.extend((last[u] + TURN_LAG, turn, (u,)) for u in ranked)
+        steps.extend((place, fold, operands) for place, operands in zip(FOLD_AT, folds))
+        steps.append((FOLDED_TURN_AT, turn, (ADDED_IN_EACH_SUM,)))
         steps.extend((place, neighbour, ug) for place, ug in enumerate(maxima))
         for place, call, arguments in sorted(steps, key=lambda step: step[0]):
             call(*arguments)

@@ -25,26 +25,15 @@ HALVES = R // BANK
 PIECES = HALVES * POINT_TILES
 LIST_COLS = J // 16
 
-ADDED_ON_VECTOR = 7
-ADDED_IN_EACH_SUM = 3
-ROUNDED_EARLY = (ADDED_ON_VECTOR, ADDED_IN_EACH_SUM)
+ADDED_ON_GPSIMD = ()
+LAST = (0, 3)
+ADDED_ON_VECTOR = ()
 SCALAR_BANKS, VECTOR_BANKS = 4, 4
 
-PIECE_STRIDE, NEIGHBOUR_STRIDE = 3, 5
-FIRST_LEAD = 8
-OWN_LAG = 6
-TURN_LAG = 6
-ROUND_SECOND_HALF_AT = (2, 5)
-QUANTISE_SECOND_HALF_AT = 10
-EACH_SUM_AT = (5, 7, 9, 11)
-FOLD_AT = (17, 19)
-FOLDED_TURN_AT = 21
-SPLIT_RESULTS = (2, 3)
 
-
-def load_plane(nc, plane, rows):
+def load_plane(queue, plane, rows):
     for quadrant in range(4):
-        nc.sync.dma_start(
+        queue.dma_start(
             out=plane[32 * quadrant : 32 * quadrant + 4, :],
             in_=rows[4 * quadrant : 4 * quadrant + 4, :].bitcast(I32),
         )
@@ -93,26 +82,27 @@ def tile_list_pnet_mix_none_kernel(
 
         wc_rows = wc.rearrange("(p i) r -> p i r", i=PACK)
         nc.sync.dma_start(offsets[:], offs)
-        load_plane(nc, tab_plane, tab_scales[0])
-        load_words(nc, tab_w, tab_words[0].rearrange("p t i -> p (t i)"))
+        load_plane(nc.sync, tab_plane, tab_scales[0])
         nc.sync.dma_start(out=c_raw[:], in_=c.rearrange("(p i) j -> p i j", i=PACK))
         nc.sync.dma_start(out=wc_raw[0][:], in_=wc_rows[:, :, :BANK])
+        load_plane(nc.sync, w_plane, w_scales[0])
+        load_words(nc, tab_w, tab_words[0].rearrange("p t i -> p (t i)"))
         load_words(nc, w_w, w_words[0].rearrange("p r i -> p (r i)"))
-        load_plane(nc, w_plane, w_scales[0])
         nc.sync.dma_start(out=wc_raw[1][:], in_=wc_rows[:, :, BANK:])
         load_words(nc, wd4_w, wd4_words[0])
         load_words(nc, wd8_w, wd8_words[0].rearrange("p n i -> p (n i)"))
-        load_plane(nc, wd4_plane, wd4_scales[0])
-        load_plane(nc, wd8_plane, wd8_scales[0])
+        load_plane(nc.sync, wd4_plane, wd4_scales[0])
+        load_plane(nc.sync, wd8_plane, wd8_scales[0])
 
-        nb_w = keep.tile([P, G, J], U32, name="nb_w", align_bytes=64)
+        nb_w = [keep.tile([P, J], U32, name=f"nb_w{g}", align_bytes=64) for g in range(G)]
         nb_plane = [keep.tile([P, 2 * J], U8, name=f"nb_plane{pair}", align_bytes=64) for pair in range(G // 2)]
-        entries = [offsets[:, 2 * pair * LIST_COLS : 2 * (pair + 1) * LIST_COLS] for pair in range(G // 2)]
-        for pair in range(G // 2):
-            nc.vector.tensor_copy(nb_plane[pair][:], tab_plane[:].bitcast(U8).indirect(entries[pair]))
-        for pair in range(G // 2):
-            picked = nb_w[:, 2 * pair : 2 * (pair + 1), :].rearrange("p g j -> p (g j)")
-            nc.vector.tensor_copy(picked, tab_w[:].indirect(entries[pair]))
+
+        def gather_scales(pair):
+            entries = offsets[:, 2 * pair * LIST_COLS : 2 * (pair + 1) * LIST_COLS]
+            nc.vector.tensor_copy(nb_plane[pair][:], tab_plane[:].bitcast(U8).indirect(entries))
+
+        def gather_words(g):
+            nc.vector.tensor_copy(nb_w[g][:], tab_w[:].indirect(offsets[:, g * LIST_COLS : (g + 1) * LIST_COLS]))
 
         c_w = keep.tile([P, J], U32, name="c_w", align_bytes=64)
         c_plane = keep.tile([P, J], U8, name="c_plane", align_bytes=64)
@@ -128,6 +118,12 @@ def tile_list_pnet_mix_none_kernel(
                 ACT.Copy,
             )
 
+        def round_rows_on_vector(rounded, raw, cols):
+            nc.vector.tensor_copy(
+                rounded[:, cols, :].rearrange("p (a b) i -> p a i b", b=4),
+                raw[:, :, cols].rearrange("p i (a b) -> p a i b", b=4),
+            )
+
         def quantise(words, plane, rounded, cols):
             nc.vector.quantize_mx(
                 out=words[:, cols].bitcast(FP8X4),
@@ -136,31 +132,33 @@ def tile_list_pnet_mix_none_kernel(
             )
 
         def from_bank(bank, u):
-            if u in ROUNDED_EARLY:
+            if u in summed:
                 return bank[:].rearrange("j (p a e) -> j a p e", a=2, e=2)
             return bank[:].rearrange("j (p t) -> j t p", t=PACK)
 
         def in_sbuf(columns, u):
-            if u in ROUNDED_EARLY:
+            if u in summed:
                 return columns.rearrange("j (a p e) -> j a p e", a=2, e=2)
             return columns.rearrange("j (t p) -> j t p", t=PACK)
 
-        ranked = [u for u in range(PIECES) if u != ADDED_IN_EACH_SUM]
-        pooled = {u: keep.tile([P, BANK], F32, name=f"pooled{u}") for u in ranked}
-        own = {u: keep.tile([P, BANK], F32, name=f"own{u}") for u in ranked if u != ADDED_ON_VECTOR}
-        summed = {u: keep.tile([P, BANK], BF16, name=f"summed{u}") for u in ROUNDED_EARLY}
+        pieces = [(h, jt) for h in range(HALVES) for jt in range(POINT_TILES)]
+        ranked = [u for u in [(0,0),(0,1),(1,0),(1,1),(0,2),(1,2),(1,3),(0,3)] if u != LAST]
+        pooled = {u: keep.tile([P, BANK], F32, name=f"pooled{u[0]}{u[1]}")[:] for u in ranked}
+        own = {u: keep.tile([P, BANK], F32, name=f"own{u[0]}{u[1]}") for u in ranked if u not in ADDED_ON_VECTOR}
+        summed = {u: keep.tile([P, BANK], BF16, name=f"summed{u[0]}{u[1]}") for u in (LAST, *ADDED_ON_GPSIMD, *ADDED_ON_VECTOR)}
         four_sums = keep.tile([P, G, BANK], BF16, name="four_sums")
         two_sums = keep.tile([P, G // 2, BANK], BF16, name="two_sums")
-        h_bf = [keep.tile([P, J, PACK], BF16, name=f"h_bf{h}", align_bytes=64) for h in range(HALVES)]
-        h_w = [keep.tile([P, J], U32, name=f"h_w{h}", align_bytes=64) for h in range(HALVES)]
-        h_plane = [keep.tile([P, J], U8, name=f"h_plane{h}", align_bytes=64) for h in range(HALVES)]
+        h_bf = {u: keep.tile([P, P, PACK], BF16, name=f"h_bf{u[0]}{u[1]}", align_bytes=64) for u in pieces}
+        h_w = {u: keep.tile([P, P], U32, name=f"h_w{u[0]}{u[1]}", align_bytes=64) for u in pieces}
+        h_plane = {u: keep.tile([P, P], U8, name=f"h_plane{u[0]}{u[1]}", align_bytes=64) for u in pieces}
 
         def neighbour_pass(bank, u, g, start):
-            h, jt = divmod(u, POINT_TILES)
+            h, jt = u
+            points = slice(jt * P, (jt + 1) * P)
             first = (g % 2) * J + jt * P
             nc.tensor.matmul_mx(
                 out=bank[:],
-                lhsT=nb_w[:, g, jt * P : (jt + 1) * P].bitcast(FP8X4),
+                lhsT=nb_w[g][:, points].bitcast(FP8X4),
                 lhsT_scale=nb_plane[g // 2][:, first : first + P],
                 rhs=w_w[:, h * BANK : (h + 1) * BANK].bitcast(FP8X4),
                 rhs_scale=w_plane[:].bitcast(U8)[:, h * BANK : (h + 1) * BANK],
@@ -169,7 +167,7 @@ def tile_list_pnet_mix_none_kernel(
             )
 
         def own_pass(bank, u, stop):
-            h, jt = divmod(u, POINT_TILES)
+            h, jt = u
             nc.tensor.matmul_mx(
                 out=bank[:],
                 lhsT=c_w[:, jt * P : (jt + 1) * P].bitcast(FP8X4),
@@ -181,47 +179,44 @@ def tile_list_pnet_mix_none_kernel(
             )
 
         def neighbour(u, g):
+            if u == LAST:
+                bank = next_bank("scalar")
+                own_pass(bank, u, False)
+                neighbour_pass(bank, u, g, False)
+                nc.scalar.activation(in_sbuf(four_sums[:, g, :], u), from_bank(bank, u), ACT.Relu)
+                return
             bank = next_bank("scalar" if g == 0 else "vector")
             neighbour_pass(bank, u, g, True)
-            running = in_sbuf(pooled[u][:], u)
+            before = after = in_sbuf(pooled[u], u)
             if g == 0:
-                nc.scalar.activation(running, from_bank(bank, u), ACT.Copy)
+                nc.scalar.activation(after, from_bank(bank, u), ACT.Copy)
             else:
-                nc.vector.tensor_tensor(running, from_bank(bank, u), running, ALU.max)
+                nc.vector.tensor_tensor(after, from_bank(bank, u), before, ALU.max)
 
         def own_part(u):
-            bank = next_bank("vector" if u == ADDED_ON_VECTOR else "scalar")
+            bank = next_bank("vector" if u in ADDED_ON_VECTOR else "scalar")
             own_pass(bank, u, True)
-            if u == ADDED_ON_VECTOR:
-                nc.vector.tensor_tensor(in_sbuf(summed[u][:], u), from_bank(bank, u), in_sbuf(pooled[u][:], u), ALU.add)
+            if u in ADDED_ON_VECTOR:
+                nc.vector.tensor_tensor(in_sbuf(summed[u][:], u), from_bank(bank, u), in_sbuf(pooled[u], u), ALU.add)
             else:
                 nc.scalar.activation(in_sbuf(own[u][:], u), from_bank(bank, u), ACT.Copy)
 
-        def neighbour_with_own_part(g):
-            bank = next_bank("scalar")
-            own_pass(bank, ADDED_IN_EACH_SUM, False)
-            neighbour_pass(bank, ADDED_IN_EACH_SUM, g, False)
-            nc.scalar.activation(
-                in_sbuf(four_sums[:, g, :], ADDED_IN_EACH_SUM), from_bank(bank, ADDED_IN_EACH_SUM), ACT.Relu
-            )
-
-        def fold(result, lower, upper):
-            nc.vector.tensor_tensor(result, lower, upper, ALU.max)
+        def add_on_gpsimd(u):
+            nc.gpsimd.tensor_tensor(summed[u][:], pooled[u], own[u][:], ALU.add)
 
         def turn(u):
-            h, jt = divmod(u, POINT_TILES)
-            rounded = h_bf[h][:, jt * P : (jt + 1) * P, :]
-            if u in ROUNDED_EARLY:
+            rounded = h_bf[u]
+            if u in summed:
                 turned = next_bank("scalar")[:, : 2 * P].rearrange("p (a j) -> p a j", a=2)
                 pairs = summed[u][:].bitcast(F32)
                 for a in range(2):
                     nc.tensor.transpose(turned[:, a, :], pairs[:, a * P : (a + 1) * P], ident[:])
-                if u == ADDED_IN_EACH_SUM:
-                    rounded_pairs = rounded.rearrange("p j t -> p (j t)").bitcast(F32)
-                    nc.scalar.copy(rounded_pairs.rearrange("p (j a) -> p j a", a=2), turned.rearrange("p a j -> p j a"))
+                if u == LAST:
+                    rounded_pairs = rounded[:].rearrange("p j t -> p (j t)").bitcast(F32)
+                    nc.vector.tensor_copy(rounded_pairs.rearrange("p (j a) -> p j a", a=2), turned.rearrange("p a j -> p j a"))
                 else:
                     nc.scalar.activation(
-                        rounded.rearrange("p j (a e) -> p j a e", e=2),
+                        rounded[:].rearrange("p j (a e) -> p j a e", e=2),
                         turned.bitcast(BF16).rearrange("p a (j e) -> p j a e", e=2),
                         ACT.Relu,
                     )
@@ -229,19 +224,22 @@ def tile_list_pnet_mix_none_kernel(
                 turned = next_bank("scalar")[:].rearrange("p (t j) -> p t j", t=PACK)
                 for t in range(PACK):
                     cols = slice(t * P, (t + 1) * P)
-                    for term, start in ((own[u], True), (pooled[u], False)):
+                    for term, start in ((pooled[u], True), (own[u][:], False)):
                         nc.tensor.matmul(
                             turned[:, t, :], term[:, cols], ident[:], start=start, stop=not start, is_transpose=True
                         )
-                nc.scalar.activation(rounded, turned.rearrange("p t j -> p j t"), ACT.Relu)
+                nc.scalar.activation(rounded[:], turned.rearrange("p t j -> p j t"), ACT.Relu)
 
-        def result_passes(y, nt, points):
+        def quantise_h(u):
+            quantise(h_w[u], h_plane[u], h_bf[u], slice(0, P))
+
+        def result_passes(y, nt, jt):
             nc.tensor.matmul_mx(
                 out=y,
                 lhsT=wd8_w[:, nt * P : (nt + 1) * P].bitcast(FP8X4),
                 lhsT_scale=wd8_plane[:].bitcast(U8)[:, nt * P : (nt + 1) * P],
-                rhs=h_w[0][:, points].bitcast(FP8X4),
-                rhs_scale=h_plane[0][:, points],
+                rhs=h_w[0, jt][:].bitcast(FP8X4),
+                rhs_scale=h_plane[0, jt][:],
                 start=True,
                 stop=False,
             )
@@ -249,66 +247,65 @@ def tile_list_pnet_mix_none_kernel(
                 out=y,
                 lhsT=wd4_w[:, 2 * nt * P : 2 * (nt + 1) * P].bitcast(FP4X4),
                 lhsT_scale=wd4_plane[:].bitcast(U8)[:, nt * P : (nt + 1) * P],
-                rhs=h_w[1][:, points].bitcast(FP8X4),
-                rhs_scale=h_plane[1][:, points],
+                rhs=h_w[1, jt][:].bitcast(FP8X4),
+                rhs_scale=h_plane[1, jt][:],
                 start=False,
                 stop=True,
             )
 
-        def second_layer(jt):
+        def second_layer(jt, reader):
             points = slice(jt * P, (jt + 1) * P)
-            quantise(h_w[1], h_plane[1], h_bf[1], points)
             y_sb = keep.tile([P, N // P, P], F32, name=f"y_sb{jt}")
-            if jt in SPLIT_RESULTS:
+            if reader == "both":
                 upper = next_bank("vector")[:, :P]
-                result_passes(upper, 0, points)
+                result_passes(upper, 0, jt)
+                lower = next_bank("vector")[:, :P]
+                result_passes(lower, 1, jt)
                 nc.vector.tensor_copy(y_sb[:, 0, :], upper)
                 nc.sync.dma_start(out=out[:P, points], in_=y_sb[:, 0, :])
-                lower = next_bank("vector")[:, :P]
-                result_passes(lower, 1, points)
                 nc.scalar.activation(y_sb[:, 1, :], lower, ACT.Copy)
                 nc.scalar.dma_start(out=out[P:, points], in_=y_sb[:, 1, :])
-            else:
-                y = next_bank("vector")[:, :N].rearrange("n (nt j) -> n nt j", j=P)
-                for nt in range(N // P):
-                    result_passes(y[:, nt, :], nt, points)
+                return
+            y = next_bank("vector")[:, :N].rearrange("n (nt j) -> n nt j", j=P)
+            for nt in range(N // P):
+                result_passes(y[:, nt, :], nt, jt)
+            if reader == "scalar":
                 nc.scalar.activation(y_sb[:], y, ACT.Copy)
-                nc.sync.dma_start(out=out[:, points].rearrange("(nt n) j -> n nt j", n=P), in_=y_sb[:])
+            else:
+                nc.vector.tensor_copy(y_sb[:], y)
+            nc.sync.dma_start(out=out[:, points].rearrange("(nt n) j -> n nt j", n=P), in_=y_sb[:])
 
         whole = slice(0, BANK)
+        for pair in range(G // 2):
+            gather_scales(pair)
         round_rows(c_bf, c_raw, whole)
         quantise(c_w, c_plane, c_bf, whole)
-        round_rows(wc_bf[0], wc_raw[0], whole)
+        round_rows(wc_bf[0], wc_raw[0], slice(0, BANK - 256))
+        if 256:
+            round_rows_on_vector(wc_bf[0], wc_raw[0], slice(BANK - 256, BANK))
         quantise(wc_w[0], wc_plane[0], wc_bf[0], whole)
-
-        maxima = sorted(
-            ((u, g) for u in ranked for g in range(1, G)),
-            key=lambda ug: (PIECE_STRIDE * ranked.index(ug[0]) + NEIGHBOUR_STRIDE * ug[1], ug[0]),
-        )
+        for g in range(G):
+            gather_words(g)
+        maxima = sorted(((u, g) for u in ranked for g in range(1, G)), key=lambda ug: (3 * ranked.index(ug[0]) + 2 * ug[1], ranked.index(ug[0])))
         last = {u: place for place, (u, g) in enumerate(maxima)}
-        parts = (slice(0, BANK // 2), slice(BANK // 2, BANK))
-        folds = (
-            (two_sums[:], four_sums[:, :2, :], four_sums[:, 2:, :]),
-            (summed[ADDED_IN_EACH_SUM][:], two_sums[:, 0, :], two_sums[:, 1, :]),
-        )
-        steps = [
-            (place, round_rows, (wc_bf[1], wc_raw[1], part)) for place, part in zip(ROUND_SECOND_HALF_AT, parts)
-        ]
-        steps.append((QUANTISE_SECOND_HALF_AT, quantise, (wc_w[1], wc_plane[1], wc_bf[1], whole)))
-        steps.extend((PIECE_STRIDE * rank - FIRST_LEAD, neighbour, (u, 0)) for rank, u in enumerate(ranked))
-        steps.extend((place, neighbour_with_own_part, (g,)) for g, place in enumerate(EACH_SUM_AT))
-        steps.extend(
-            (last[u] + 1 if u == ADDED_ON_VECTOR else PIECE_STRIDE * rank + OWN_LAG, own_part, (u,))
-            for rank, u in enumerate(ranked)
-        )
-        steps.extend((last[u] + TURN_LAG, turn, (u,)) for u in ranked)
-        steps.extend((place, fold, operands) for place, operands in zip(FOLD_AT, folds))
-        steps.append((FOLDED_TURN_AT, turn, (ADDED_IN_EACH_SUM,)))
+        end = len(maxima)
+        steps = [(-9, own_part, (u,)) for u in ranked if u[0] == 0 and ranked.index(u) < 5]
+        steps.extend((-8, neighbour, (u, 0)) for u in ranked[:4])
+        steps.extend((-7, round_rows, (wc_bf[1], wc_raw[1], slice(a * BANK // 1, (a + 1) * BANK // 1))) for a in range(1))
+        steps.append((3, quantise, (wc_w[1], wc_plane[1], wc_bf[1], whole)))
+        steps.extend((3 * rank - 3, neighbour, (u, 0)) for rank, u in enumerate(ranked) if rank >= 4)
+        steps.extend((max(3, last[u] + 1), own_part, (u,)) for u in ranked if u[0] == 1 or ranked.index(u) >= 5)
+        steps.extend((0 + 2 * g, neighbour, (LAST, g)) for g in range(G))
+        steps.extend((max(last[u] + 1, last[u] + 1), add_on_gpsimd, (u,)) for u in ADDED_ON_GPSIMD)
+        turnat = {u: last[u] + (5 if u in ADDED_ON_GPSIMD else 5) for u in ranked}
+        turnat[LAST] = end + 3
+        steps.append((end + 0, nc.vector.tensor_tensor, (two_sums[:], four_sums[:, :2, :], four_sums[:, 2:, :], ALU.max)))
+        steps.append((end + 0, nc.vector.tensor_tensor, (summed[LAST][:], two_sums[:, 0, :], two_sums[:, 1, :], ALU.max)))
+        steps.extend((turnat[u], turn, (u,)) for u in turnat)
+        qat = {u: max(last[u] + 13, turnat[u]) for u in ranked}
+        qat[LAST] = end + 3 + 1
+        steps.extend((qat[u], quantise_h, (u,)) for u in qat)
+        steps.extend((max(qat[0, jt], qat[1, jt]) + 0, second_layer, (jt, ("scalar","scalar","scalar","both")[jt])) for jt in range(POINT_TILES))
         steps.extend((place, neighbour, ug) for place, ug in enumerate(maxima))
         for place, call, arguments in sorted(steps, key=lambda step: step[0]):
             call(*arguments)
-
-        for points in (slice(0, J // 2), slice(J // 2, J)):
-            quantise(h_w[0], h_plane[0], h_bf[0], points)
-        for jt in range(POINT_TILES):
-            second_layer(jt)

@@ -25,9 +25,10 @@ HALVES = R // BANK
 PIECES = HALVES * POINT_TILES
 LIST_COLS = J // 16
 
-ADDED_ON_GPSIMD = ()
+ADDED_ON_GPSIMD = ((0, 1), (1, 0), (1, 1), (0, 2),)
 LAST = (0, 3)
 ADDED_ON_VECTOR = ()
+RELU_ON_VECTOR = ()
 SCALAR_BANKS, VECTOR_BANKS = 4, 4
 
 
@@ -83,11 +84,11 @@ def tile_list_pnet_mix_none_kernel(
         wc_rows = wc.rearrange("(p i) r -> p i r", i=PACK)
         nc.sync.dma_start(offsets[:], offs)
         load_plane(nc.sync, tab_plane, tab_scales[0])
+        load_words(nc, tab_w, tab_words[0].rearrange("p t i -> p (t i)"))
         nc.sync.dma_start(out=c_raw[:], in_=c.rearrange("(p i) j -> p i j", i=PACK))
         nc.sync.dma_start(out=wc_raw[0][:], in_=wc_rows[:, :, :BANK])
-        load_plane(nc.sync, w_plane, w_scales[0])
-        load_words(nc, tab_w, tab_words[0].rearrange("p t i -> p (t i)"))
         load_words(nc, w_w, w_words[0].rearrange("p r i -> p (r i)"))
+        load_plane(nc.sync, w_plane, w_scales[0])
         nc.sync.dma_start(out=wc_raw[1][:], in_=wc_rows[:, :, BANK:])
         load_words(nc, wd4_w, wd4_words[0])
         load_words(nc, wd8_w, wd8_words[0].rearrange("p n i -> p (n i)"))
@@ -142,7 +143,7 @@ def tile_list_pnet_mix_none_kernel(
             return columns.rearrange("j (t p) -> j t p", t=PACK)
 
         pieces = [(h, jt) for h in range(HALVES) for jt in range(POINT_TILES)]
-        ranked = [u for u in [(0,0),(0,1),(1,0),(1,1),(0,2),(1,2),(1,3),(0,3)] if u != LAST]
+        ranked = [u for u in ((0, 0), (0, 1), (1, 0), (1, 1), (0, 2), (1, 2), (1, 3), (0, 3),) if u != LAST]
         pooled = {u: keep.tile([P, BANK], F32, name=f"pooled{u[0]}{u[1]}")[:] for u in ranked}
         own = {u: keep.tile([P, BANK], F32, name=f"own{u[0]}{u[1]}") for u in ranked if u not in ADDED_ON_VECTOR}
         summed = {u: keep.tile([P, BANK], BF16, name=f"summed{u[0]}{u[1]}") for u in (LAST, *ADDED_ON_GPSIMD, *ADDED_ON_VECTOR)}
@@ -213,7 +214,7 @@ def tile_list_pnet_mix_none_kernel(
                     nc.tensor.transpose(turned[:, a, :], pairs[:, a * P : (a + 1) * P], ident[:])
                 if u == LAST:
                     rounded_pairs = rounded[:].rearrange("p j t -> p (j t)").bitcast(F32)
-                    nc.vector.tensor_copy(rounded_pairs.rearrange("p (j a) -> p j a", a=2), turned.rearrange("p a j -> p j a"))
+                    nc.scalar.copy(rounded_pairs.rearrange("p (j a) -> p j a", a=2), turned.rearrange("p a j -> p j a"))
                 else:
                     nc.scalar.activation(
                         rounded[:].rearrange("p j (a e) -> p j a e", e=2),
@@ -228,7 +229,10 @@ def tile_list_pnet_mix_none_kernel(
                         nc.tensor.matmul(
                             turned[:, t, :], term[:, cols], ident[:], start=start, stop=not start, is_transpose=True
                         )
-                nc.scalar.activation(rounded[:], turned.rearrange("p t j -> p j t"), ACT.Relu)
+                if u in RELU_ON_VECTOR:
+                    nc.vector.tensor_scalar(rounded[:], turned.rearrange("p t j -> p j t"), 0.0, None, ALU.max)
+                else:
+                    nc.scalar.activation(rounded[:], turned.rearrange("p t j -> p j t"), ACT.Relu)
 
         def quantise_h(u):
             quantise(h_w[u], h_plane[u], h_bf[u], slice(0, P))
@@ -266,7 +270,7 @@ def tile_list_pnet_mix_none_kernel(
                 nc.scalar.activation(y_sb[:, 1, :], lower, ACT.Copy)
                 nc.scalar.dma_start(out=out[P:, points], in_=y_sb[:, 1, :])
                 return
-            y = next_bank("vector")[:, :N].rearrange("n (nt j) -> n nt j", j=P)
+            y = next_bank("scalar")[:, :N].rearrange("n (nt j) -> n nt j", j=P)
             for nt in range(N // P):
                 result_passes(y[:, nt, :], nt, jt)
             if reader == "scalar":
@@ -280,32 +284,34 @@ def tile_list_pnet_mix_none_kernel(
             gather_scales(pair)
         round_rows(c_bf, c_raw, whole)
         quantise(c_w, c_plane, c_bf, whole)
-        round_rows(wc_bf[0], wc_raw[0], slice(0, BANK - 256))
-        if 256:
-            round_rows_on_vector(wc_bf[0], wc_raw[0], slice(BANK - 256, BANK))
+        round_rows(wc_bf[0], wc_raw[0], slice(0, BANK - 0))
+        if 0:
+            round_rows_on_vector(wc_bf[0], wc_raw[0], slice(BANK - 0, BANK))
         quantise(wc_w[0], wc_plane[0], wc_bf[0], whole)
         for g in range(G):
             gather_words(g)
         maxima = sorted(((u, g) for u in ranked for g in range(1, G)), key=lambda ug: (3 * ranked.index(ug[0]) + 2 * ug[1], ranked.index(ug[0])))
         last = {u: place for place, (u, g) in enumerate(maxima)}
         end = len(maxima)
-        steps = [(-9, own_part, (u,)) for u in ranked if u[0] == 0 and ranked.index(u) < 5]
+        steps = [(-9, own_part, (u,)) for u in ranked if u[0] == 0 and ranked.index(u) < 0]
         steps.extend((-8, neighbour, (u, 0)) for u in ranked[:4])
         steps.extend((-7, round_rows, (wc_bf[1], wc_raw[1], slice(a * BANK // 1, (a + 1) * BANK // 1))) for a in range(1))
-        steps.append((3, quantise, (wc_w[1], wc_plane[1], wc_bf[1], whole)))
-        steps.extend((3 * rank - 3, neighbour, (u, 0)) for rank, u in enumerate(ranked) if rank >= 4)
-        steps.extend((max(3, last[u] + 1), own_part, (u,)) for u in ranked if u[0] == 1 or ranked.index(u) >= 5)
-        steps.extend((0 + 2 * g, neighbour, (LAST, g)) for g in range(G))
+        steps.append((1, quantise, (wc_w[1], wc_plane[1], wc_bf[1], whole)))
+        steps.extend((3 * rank - 5, neighbour, (u, 0)) for rank, u in enumerate(ranked) if rank >= 4)
+        steps.extend((last[u] + 1 if u in ADDED_ON_VECTOR else max(1, min(last[u] + 1, 99)), own_part, (u,)) for u in ranked if u[0] == 1 or ranked.index(u) >= 0)
+        steps.extend((5 + 5 * g, neighbour, (LAST, g)) for g in range(G))
         steps.extend((max(last[u] + 1, last[u] + 1), add_on_gpsimd, (u,)) for u in ADDED_ON_GPSIMD)
-        turnat = {u: last[u] + (5 if u in ADDED_ON_GPSIMD else 5) for u in ranked}
-        turnat[LAST] = end + 3
+        turnat = {u: last[u] + (9 if u in ADDED_ON_GPSIMD else 6) for u in ranked}
+        for rank in ():
+            turnat[ranked[rank]] = turnat[ranked[rank + 1]]
+        turnat[LAST] = end + 5
         steps.append((end + 0, nc.vector.tensor_tensor, (two_sums[:], four_sums[:, :2, :], four_sums[:, 2:, :], ALU.max)))
-        steps.append((end + 0, nc.vector.tensor_tensor, (summed[LAST][:], two_sums[:, 0, :], two_sums[:, 1, :], ALU.max)))
+        steps.append((end + 2, nc.vector.tensor_tensor, (summed[LAST][:], two_sums[:, 0, :], two_sums[:, 1, :], ALU.max)))
         steps.extend((turnat[u], turn, (u,)) for u in turnat)
-        qat = {u: max(last[u] + 13, turnat[u]) for u in ranked}
-        qat[LAST] = end + 3 + 1
+        qat = {u: max(min(26, last[u] + 30), turnat[u] + 0) for u in ranked}
+        qat[LAST] = end + 5 + 1
         steps.extend((qat[u], quantise_h, (u,)) for u in qat)
-        steps.extend((max(qat[0, jt], qat[1, jt]) + 0, second_layer, (jt, ("scalar","scalar","scalar","both")[jt])) for jt in range(POINT_TILES))
+        steps.extend((max(qat[0, jt], qat[1, jt]) + 3, second_layer, (jt, ("scalar","scalar","both","both")[jt])) for jt in range(POINT_TILES))
         steps.extend((place, neighbour, ug) for place, ug in enumerate(maxima))
         for place, call, arguments in sorted(steps, key=lambda step: step[0]):
             call(*arguments)

@@ -28,7 +28,8 @@ LIST_COLS = J // 16
 ADDED_ON_GPSIMD = ((0, 1), (1, 0), (1, 1), (0, 2),)
 LAST = (0, 3)
 ADDED_ON_VECTOR = ()
-RELU_ON_VECTOR = ()
+MERGED = ((0, 1),)
+RELU_ON_VECTOR = ((0, 2),)
 SCALAR_BANKS, VECTOR_BANKS = 4, 4
 
 
@@ -95,7 +96,8 @@ def tile_list_pnet_mix_none_kernel(
         load_plane(nc.sync, wd4_plane, wd4_scales[0])
         load_plane(nc.sync, wd8_plane, wd8_scales[0])
 
-        nb_w = [keep.tile([P, J], U32, name=f"nb_w{g}", align_bytes=64) for g in range(G)]
+        nb_pair = [keep.tile([P, 2 * J], U32, name=f"nb_w{pair}", align_bytes=64) for pair in range(G // 2)]
+        nb_w = [nb_pair[g // 2][:, (g % 2) * J : (g % 2 + 1) * J] for g in range(G)]
         nb_plane = [keep.tile([P, 2 * J], U8, name=f"nb_plane{pair}", align_bytes=64) for pair in range(G // 2)]
 
         def gather_scales(pair):
@@ -103,13 +105,13 @@ def tile_list_pnet_mix_none_kernel(
             nc.vector.tensor_copy(nb_plane[pair][:], tab_plane[:].bitcast(U8).indirect(entries))
 
         def gather_words(g):
-            nc.vector.tensor_copy(nb_w[g][:], tab_w[:].indirect(offsets[:, g * LIST_COLS : (g + 1) * LIST_COLS]))
+            nc.vector.tensor_copy(nb_pair[g][:], tab_w[:].indirect(offsets[:, 2 * g * LIST_COLS : 2 * (g + 1) * LIST_COLS]))
 
         c_w = keep.tile([P, J], U32, name="c_w", align_bytes=64)
         c_plane = keep.tile([P, J], U8, name="c_plane", align_bytes=64)
         wc_w = [keep.tile([P, BANK], U32, name=f"wc_w{h}", align_bytes=64) for h in range(HALVES)]
         wc_plane = [keep.tile([P, BANK], U8, name=f"wc_plane{h}", align_bytes=64) for h in range(HALVES)]
-        wc_bf = [keep.tile([P, BANK, PACK], BF16, name=f"wc_bf{h}", align_bytes=64) for h in range(HALVES)]
+        wc_bf = [keep.tile([P, BANK, PACK], BF16, name="wc_bf", align_bytes=64)] * HALVES
         c_bf = keep.tile([P, J, PACK], BF16, name="c_bf", align_bytes=64)
 
         def round_rows(rounded, raw, cols):
@@ -117,6 +119,11 @@ def tile_list_pnet_mix_none_kernel(
                 rounded[:, cols, :].rearrange("p (a b) i -> p a i b", b=4),
                 raw[:, :, cols].rearrange("p i (a b) -> p a i b", b=4),
                 ACT.Copy,
+            )
+
+        def round_rows_on_gpsimd(rounded, raw, cols):
+            nc.gpsimd.tensor_scalar(
+                rounded[:, cols, :], raw[:, :, cols].rearrange("p i a -> p a i"), 1.0, 0.0, ALU.mult, ALU.add
             )
 
         def round_rows_on_vector(rounded, raw, cols):
@@ -149,9 +156,12 @@ def tile_list_pnet_mix_none_kernel(
         summed = {u: keep.tile([P, BANK], BF16, name=f"summed{u[0]}{u[1]}") for u in (LAST, *ADDED_ON_GPSIMD, *ADDED_ON_VECTOR)}
         four_sums = keep.tile([P, G, BANK], BF16, name="four_sums")
         two_sums = keep.tile([P, G // 2, BANK], BF16, name="two_sums")
-        h_bf = {u: keep.tile([P, P, PACK], BF16, name=f"h_bf{u[0]}{u[1]}", align_bytes=64) for u in pieces}
-        h_w = {u: keep.tile([P, P], U32, name=f"h_w{u[0]}{u[1]}", align_bytes=64) for u in pieces}
-        h_plane = {u: keep.tile([P, P], U8, name=f"h_plane{u[0]}{u[1]}", align_bytes=64) for u in pieces}
+        h_bf_all = [keep.tile([P, J, PACK], BF16, name=f"h_bf{h}", align_bytes=64) for h in range(HALVES)]
+        h_w_all = [keep.tile([P, J], U32, name=f"h_w{h}", align_bytes=64) for h in range(HALVES)]
+        h_plane_all = [keep.tile([P, J], U8, name=f"h_plane{h}", align_bytes=64) for h in range(HALVES)]
+        h_bf = {(h, jt): h_bf_all[h][:, jt * P : (jt + 1) * P, :] for h, jt in pieces}
+        h_w = {(h, jt): h_w_all[h][:, jt * P : (jt + 1) * P] for h, jt in pieces}
+        h_plane = {(h, jt): h_plane_all[h][:, jt * P : (jt + 1) * P] for h, jt in pieces}
 
         def neighbour_pass(bank, u, g, start):
             h, jt = u
@@ -215,6 +225,14 @@ def tile_list_pnet_mix_none_kernel(
                 if u == LAST:
                     rounded_pairs = rounded[:].rearrange("p j t -> p (j t)").bitcast(F32)
                     nc.scalar.copy(rounded_pairs.rearrange("p (j a) -> p j a", a=2), turned.rearrange("p a j -> p j a"))
+                elif u in RELU_ON_VECTOR:
+                    nc.vector.tensor_scalar(
+                        rounded[:].rearrange("p j (a e) -> p j a e", e=2),
+                        turned.bitcast(BF16).rearrange("p a (j e) -> p j a e", e=2),
+                        0.0,
+                        None,
+                        ALU.max,
+                    )
                 else:
                     nc.scalar.activation(
                         rounded[:].rearrange("p j (a e) -> p j a e", e=2),
@@ -234,8 +252,8 @@ def tile_list_pnet_mix_none_kernel(
                 else:
                     nc.scalar.activation(rounded[:], turned.rearrange("p t j -> p j t"), ACT.Relu)
 
-        def quantise_h(u):
-            quantise(h_w[u], h_plane[u], h_bf[u], slice(0, P))
+        def quantise_h(h, jt, count):
+            quantise(h_w_all[h], h_plane_all[h], h_bf_all[h], slice(jt * P, (jt + count) * P))
 
         def result_passes(y, nt, jt):
             nc.tensor.matmul_mx(
@@ -270,7 +288,7 @@ def tile_list_pnet_mix_none_kernel(
                 nc.scalar.activation(y_sb[:, 1, :], lower, ACT.Copy)
                 nc.scalar.dma_start(out=out[P:, points], in_=y_sb[:, 1, :])
                 return
-            y = next_bank("scalar")[:, :N].rearrange("n (nt j) -> n nt j", j=P)
+            y = next_bank("vector")[:, :N].rearrange("n (nt j) -> n nt j", j=P)
             for nt in range(N // P):
                 result_passes(y[:, nt, :], nt, jt)
             if reader == "scalar":
@@ -288,30 +306,36 @@ def tile_list_pnet_mix_none_kernel(
         if 0:
             round_rows_on_vector(wc_bf[0], wc_raw[0], slice(BANK - 0, BANK))
         quantise(wc_w[0], wc_plane[0], wc_bf[0], whole)
-        for g in range(G):
+        for g in range(G // 2):
             gather_words(g)
-        maxima = sorted(((u, g) for u in ranked for g in range(1, G)), key=lambda ug: (3 * ranked.index(ug[0]) + 2 * ug[1], ranked.index(ug[0])))
-        last = {u: place for place, (u, g) in enumerate(maxima)}
+        maxima = sorted(((u, g) for u in ranked for g in range(1, G)), key=lambda ug: 3 * ranked.index(ug[0]) + 2 * ug[1])
+        after = {u: place + 1 for place, (u, g) in enumerate(maxima)}
         end = len(maxima)
-        steps = [(-9, own_part, (u,)) for u in ranked if u[0] == 0 and ranked.index(u) < 0]
-        steps.extend((-8, neighbour, (u, 0)) for u in ranked[:4])
-        steps.extend((-7, round_rows, (wc_bf[1], wc_raw[1], slice(a * BANK // 1, (a + 1) * BANK // 1))) for a in range(1))
-        steps.append((1, quantise, (wc_w[1], wc_plane[1], wc_bf[1], whole)))
-        steps.extend((3 * rank - 5, neighbour, (u, 0)) for rank, u in enumerate(ranked) if rank >= 4)
-        steps.extend((last[u] + 1 if u in ADDED_ON_VECTOR else max(1, min(last[u] + 1, 99)), own_part, (u,)) for u in ranked if u[0] == 1 or ranked.index(u) >= 0)
+        for u in ranked[:3]:
+            neighbour(u, 0)
+        round_rows_on_gpsimd(wc_bf[1], wc_raw[1], slice(0, 256))
+        round_rows(wc_bf[1], wc_raw[1], slice(256, BANK))
+        steps = [(1, quantise, (wc_w[1], wc_plane[1], wc_bf[1], whole))]
+        steps.extend((3 * rank - 5, neighbour, (u, 0)) for rank, u in enumerate(ranked) if rank >= 3)
+        steps.extend((after[u], own_part, (u,)) for u in ranked)
         steps.extend((5 + 5 * g, neighbour, (LAST, g)) for g in range(G))
-        steps.extend((max(last[u] + 1, last[u] + 1), add_on_gpsimd, (u,)) for u in ADDED_ON_GPSIMD)
-        turnat = {u: last[u] + (9 if u in ADDED_ON_GPSIMD else 6) for u in ranked}
-        for rank in ():
-            turnat[ranked[rank]] = turnat[ranked[rank + 1]]
-        turnat[LAST] = end + 5
-        steps.append((end + 0, nc.vector.tensor_tensor, (two_sums[:], four_sums[:, :2, :], four_sums[:, 2:, :], ALU.max)))
-        steps.append((end + 2, nc.vector.tensor_tensor, (summed[LAST][:], two_sums[:, 0, :], two_sums[:, 1, :], ALU.max)))
-        steps.extend((turnat[u], turn, (u,)) for u in turnat)
-        qat = {u: max(min(26, last[u] + 30), turnat[u] + 0) for u in ranked}
-        qat[LAST] = end + 5 + 1
-        steps.extend((qat[u], quantise_h, (u,)) for u in qat)
-        steps.extend((max(qat[0, jt], qat[1, jt]) + 3, second_layer, (jt, ("scalar","scalar","both","both")[jt])) for jt in range(POINT_TILES))
+        steps.extend((after[u], add_on_gpsimd, (u,)) for u in ADDED_ON_GPSIMD)
+        turn_at = {u: after[u] - 1 + (9 if u in ADDED_ON_GPSIMD else 5) for u in ranked}
+        steps.extend((turn_at[u], turn, (u,)) for u in ranked if turn_at[u] <= end)
+        steps.append((end - 1, quantise_h, (0, 0, 2)))
         steps.extend((place, neighbour, ug) for place, ug in enumerate(maxima))
         for place, call, arguments in sorted(steps, key=lambda step: step[0]):
             call(*arguments)
+        nc.vector.tensor_tensor(two_sums[:], four_sums[:, :2, :], four_sums[:, 2:, :], ALU.max)
+        nc.vector.tensor_tensor(summed[LAST][:], two_sums[:, 0, :], two_sums[:, 1, :], ALU.max)
+        late = sorted((u for u in ranked if turn_at[u] > end), key=turn_at.get)
+        for u in late:
+            turn(u)
+        quantise_h(1, 0, 1)
+        second_layer(0, "scalar")
+        turn(LAST)
+        for jt in range(1, POINT_TILES):
+            if jt >= 2:
+                quantise_h(0, jt, 1)
+            quantise_h(1, jt, 1)
+            second_layer(jt, "both" if jt >= 3 else "scalar")

@@ -142,12 +142,12 @@ def tile_list_pnet_mix_none_kernel(
         def from_bank(bank, u):
             if u in summed:
                 return bank[:].rearrange("j (p a e) -> j a p e", a=2, e=2)
-            return bank[:].rearrange("j (p t) -> j t p", t=PACK)
+            return bank[:].rearrange("j (b q t) -> j b t q", q=4, t=PACK)
 
         def in_sbuf(columns, u):
             if u in summed:
                 return columns.rearrange("j (a p e) -> j a p e", a=2, e=2)
-            return columns.rearrange("j (t p) -> j t p", t=PACK)
+            return columns.rearrange("j (t b q) -> j b t q", q=4, t=PACK)
 
         pieces = [(h, jt) for h in range(HALVES) for jt in range(POINT_TILES)]
         ranked = [u for u in ((0, 0), (0, 1), (1, 0), (1, 1), (0, 2), (1, 2), (1, 3), (0, 3),) if u != LAST]

@@ -22,20 +22,28 @@ PACK = 4
 BANK = 512
 POINT_TILES = J // P
 HALVES = R // BANK
-PIECES = HALVES * POINT_TILES
-LIST_COLS = J // 16
+PAIRS = G // 2
+PAIR_COLS = 2 * J // 16
+ALIGN = 256
+BANKS_A_SET = 4
 
-ADDED_ON_GPSIMD = ((0, 1), (1, 0), (1, 1), (0, 2),)
-LAST = (0, 3)
-ADDED_ON_VECTOR = ()
-MERGED = ((0, 1),)
-RELU_ON_VECTOR = ((0, 2),)
-SCALAR_BANKS, VECTOR_BANKS = 4, 4
+RANKED = ((0, 0), (0, 1), (1, 0), (1, 1), (0, 2), (1, 2), (1, 3))
+IN_EACH_SUM = (0, 3)
+ON_GPSIMD = RANKED[1:-2]
+LAST_SUM_APART = ON_GPSIMD[-1]
+AS_PAIRS = (IN_EACH_SUM, *ON_GPSIMD)
+GPSIMD_COLUMNS = 256
+
+FIRST_LEAD = 8
+EACH_SUM_STEP = 5
+LAST_SUM_LAG = 3
+TURN_LAG = BANKS_A_SET + 1
+TURN_LAG_GPSIMD = 10
 
 
-def load_plane(queue, plane, rows):
+def load_plane(nc, plane, rows):
     for quadrant in range(4):
-        queue.dma_start(
+        nc.sync.dma_start(
             out=plane[32 * quadrant : 32 * quadrant + 4, :],
             in_=rows[4 * quadrant : 4 * quadrant + 4, :].bitcast(I32),
         )
@@ -53,24 +61,24 @@ def tile_list_pnet_mix_none_kernel(
         keep = ctx.enter_context(tc.tile_pool(name="keep", bufs=1))
         psum = ctx.enter_context(tc.psum_pool(name="psum", bufs=1))
 
-        banks = [psum.tile([P, BANK], F32, name=f"bank{b}") for b in range(SCALAR_BANKS + VECTOR_BANKS)]
-        bank_sets = {"scalar": banks[:SCALAR_BANKS], "vector": banks[SCALAR_BANKS:]}
+        banks = [psum.tile([P, BANK], F32, name=f"bank{b}") for b in range(2 * BANKS_A_SET)]
+        bank_sets = {"scalar": banks[:BANKS_A_SET], "vector": banks[BANKS_A_SET:]}
         taken = {"scalar": [], "vector": []}
 
-        def next_bank(reader):
-            bank = bank_sets[reader][len(taken[reader]) % len(bank_sets[reader])]
-            taken[reader].append(bank)
+        def next_bank(which):
+            bank = bank_sets[which][len(taken[which]) % BANKS_A_SET]
+            taken[which].append(bank)
             return bank
 
-        offsets = keep.tile([P, G * LIST_COLS], U16, name="offsets")
-        tab_plane = keep.tile([P, T // 4], I32, name="tab_plane", align_bytes=64)
-        w_plane = keep.tile([P, R // 4], I32, name="w_plane", align_bytes=64)
-        wd8_plane = keep.tile([P, N // 4], I32, name="wd8_plane", align_bytes=64)
-        wd4_plane = keep.tile([P, N // 4], I32, name="wd4_plane", align_bytes=64)
-        tab_w = keep.tile([P, T], U32, name="tab_w", align_bytes=64)
-        w_w = keep.tile([P, R], U32, name="w_w", align_bytes=64)
-        wd8_w = keep.tile([P, N], U32, name="wd8_w", align_bytes=64)
-        wd4_w = keep.tile([P, 2 * N], U8, name="wd4_w", align_bytes=64)
+        offsets = keep.tile([P, PAIRS * PAIR_COLS], U16, name="offsets")
+        tab_plane = keep.tile([P, T // 4], I32, name="tab_plane", align_bytes=ALIGN)
+        w_plane = keep.tile([P, R // 4], I32, name="w_plane", align_bytes=ALIGN)
+        wd8_plane = keep.tile([P, N // 4], I32, name="wd8_plane", align_bytes=ALIGN)
+        wd4_plane = keep.tile([P, N // 4], I32, name="wd4_plane", align_bytes=ALIGN)
+        tab_w = keep.tile([P, T], U32, name="tab_w", align_bytes=ALIGN)
+        w_w = keep.tile([P, R], U32, name="w_w", align_bytes=ALIGN)
+        wd8_w = keep.tile([P, N], U32, name="wd8_w", align_bytes=ALIGN)
+        wd4_w = keep.tile([P, 2 * N], U8, name="wd4_w", align_bytes=ALIGN)
         c_raw = keep.tile([P, PACK, J], F32, name="c_raw")
         wc_raw = [keep.tile([P, PACK, BANK], F32, name=f"wc_raw{h}") for h in range(HALVES)]
         ident = keep.tile([P, P], F32, name="ident")
@@ -84,35 +92,28 @@ def tile_list_pnet_mix_none_kernel(
 
         wc_rows = wc.rearrange("(p i) r -> p i r", i=PACK)
         nc.sync.dma_start(offsets[:], offs)
-        load_plane(nc.sync, tab_plane, tab_scales[0])
+        load_plane(nc, tab_plane, tab_scales[0])
         load_words(nc, tab_w, tab_words[0].rearrange("p t i -> p (t i)"))
         nc.sync.dma_start(out=c_raw[:], in_=c.rearrange("(p i) j -> p i j", i=PACK))
         nc.sync.dma_start(out=wc_raw[0][:], in_=wc_rows[:, :, :BANK])
         load_words(nc, w_w, w_words[0].rearrange("p r i -> p (r i)"))
-        load_plane(nc.sync, w_plane, w_scales[0])
+        load_plane(nc, w_plane, w_scales[0])
         nc.sync.dma_start(out=wc_raw[1][:], in_=wc_rows[:, :, BANK:])
         load_words(nc, wd4_w, wd4_words[0])
         load_words(nc, wd8_w, wd8_words[0].rearrange("p n i -> p (n i)"))
-        load_plane(nc.sync, wd4_plane, wd4_scales[0])
-        load_plane(nc.sync, wd8_plane, wd8_scales[0])
+        load_plane(nc, wd4_plane, wd4_scales[0])
+        load_plane(nc, wd8_plane, wd8_scales[0])
 
-        nb_pair = [keep.tile([P, 2 * J], U32, name=f"nb_w{pair}", align_bytes=64) for pair in range(G // 2)]
-        nb_w = [nb_pair[g // 2][:, (g % 2) * J : (g % 2 + 1) * J] for g in range(G)]
-        nb_plane = [keep.tile([P, 2 * J], U8, name=f"nb_plane{pair}", align_bytes=64) for pair in range(G // 2)]
+        nb_w = [keep.tile([P, 2 * J], U32, name=f"nb_w{pair}", align_bytes=ALIGN) for pair in range(PAIRS)]
+        nb_plane = [keep.tile([P, 2 * J], U8, name=f"nb_plane{pair}", align_bytes=ALIGN) for pair in range(PAIRS)]
+        entries = [offsets[:, pair * PAIR_COLS : (pair + 1) * PAIR_COLS] for pair in range(PAIRS)]
 
-        def gather_scales(pair):
-            entries = offsets[:, 2 * pair * LIST_COLS : 2 * (pair + 1) * LIST_COLS]
-            nc.vector.tensor_copy(nb_plane[pair][:], tab_plane[:].bitcast(U8).indirect(entries))
-
-        def gather_words(g):
-            nc.vector.tensor_copy(nb_pair[g][:], tab_w[:].indirect(offsets[:, 2 * g * LIST_COLS : 2 * (g + 1) * LIST_COLS]))
-
-        c_w = keep.tile([P, J], U32, name="c_w", align_bytes=64)
-        c_plane = keep.tile([P, J], U8, name="c_plane", align_bytes=64)
-        wc_w = [keep.tile([P, BANK], U32, name=f"wc_w{h}", align_bytes=64) for h in range(HALVES)]
-        wc_plane = [keep.tile([P, BANK], U8, name=f"wc_plane{h}", align_bytes=64) for h in range(HALVES)]
-        wc_bf = [keep.tile([P, BANK, PACK], BF16, name="wc_bf", align_bytes=64)] * HALVES
-        c_bf = keep.tile([P, J, PACK], BF16, name="c_bf", align_bytes=64)
+        c_w = keep.tile([P, J], U32, name="c_w", align_bytes=ALIGN)
+        c_plane = keep.tile([P, J], U8, name="c_plane", align_bytes=ALIGN)
+        wc_w = [keep.tile([P, BANK], U32, name=f"wc_w{h}", align_bytes=ALIGN) for h in range(HALVES)]
+        wc_plane = [keep.tile([P, BANK], U8, name=f"wc_plane{h}", align_bytes=ALIGN) for h in range(HALVES)]
+        wc_bf = keep.tile([P, BANK, PACK], BF16, name="wc_bf", align_bytes=ALIGN)
+        c_bf = keep.tile([P, J, PACK], BF16, name="c_bf", align_bytes=ALIGN)
 
         def round_rows(rounded, raw, cols):
             nc.scalar.activation(
@@ -126,12 +127,6 @@ def tile_list_pnet_mix_none_kernel(
                 rounded[:, cols, :], raw[:, :, cols].rearrange("p i a -> p a i"), 1.0, 0.0, ALU.mult, ALU.add
             )
 
-        def round_rows_on_vector(rounded, raw, cols):
-            nc.vector.tensor_copy(
-                rounded[:, cols, :].rearrange("p (a b) i -> p a i b", b=4),
-                raw[:, :, cols].rearrange("p i (a b) -> p a i b", b=4),
-            )
-
         def quantise(words, plane, rounded, cols):
             nc.vector.quantize_mx(
                 out=words[:, cols].bitcast(FP8X4),
@@ -140,37 +135,32 @@ def tile_list_pnet_mix_none_kernel(
             )
 
         def from_bank(bank, u):
-            if u in summed:
+            if u in AS_PAIRS:
                 return bank[:].rearrange("j (p a e) -> j a p e", a=2, e=2)
             return bank[:].rearrange("j (b q t) -> j b t q", q=4, t=PACK)
 
         def in_sbuf(columns, u):
-            if u in summed:
+            if u in AS_PAIRS:
                 return columns.rearrange("j (a p e) -> j a p e", a=2, e=2)
             return columns.rearrange("j (t b q) -> j b t q", q=4, t=PACK)
 
-        pieces = [(h, jt) for h in range(HALVES) for jt in range(POINT_TILES)]
-        ranked = [u for u in ((0, 0), (0, 1), (1, 0), (1, 1), (0, 2), (1, 2), (1, 3), (0, 3),) if u != LAST]
-        pooled = {u: keep.tile([P, BANK], F32, name=f"pooled{u[0]}{u[1]}")[:] for u in ranked}
-        own = {u: keep.tile([P, BANK], F32, name=f"own{u[0]}{u[1]}") for u in ranked if u not in ADDED_ON_VECTOR}
-        summed = {u: keep.tile([P, BANK], BF16, name=f"summed{u[0]}{u[1]}") for u in (LAST, *ADDED_ON_GPSIMD, *ADDED_ON_VECTOR)}
+        pooled = {u: keep.tile([P, BANK], F32, name=f"pooled{u[0]}{u[1]}") for u in RANKED}
+        own = {u: keep.tile([P, BANK], F32, name=f"own{u[0]}{u[1]}") for u in RANKED}
+        summed = {u: keep.tile([P, BANK], BF16, name=f"summed{u[0]}{u[1]}") for u in AS_PAIRS}
+        last_sum = keep.tile([P, BANK], BF16, name="last_sum")
         four_sums = keep.tile([P, G, BANK], BF16, name="four_sums")
         two_sums = keep.tile([P, G // 2, BANK], BF16, name="two_sums")
-        h_bf_all = [keep.tile([P, J, PACK], BF16, name=f"h_bf{h}", align_bytes=64) for h in range(HALVES)]
-        h_w_all = [keep.tile([P, J], U32, name=f"h_w{h}", align_bytes=64) for h in range(HALVES)]
-        h_plane_all = [keep.tile([P, J], U8, name=f"h_plane{h}", align_bytes=64) for h in range(HALVES)]
-        h_bf = {(h, jt): h_bf_all[h][:, jt * P : (jt + 1) * P, :] for h, jt in pieces}
-        h_w = {(h, jt): h_w_all[h][:, jt * P : (jt + 1) * P] for h, jt in pieces}
-        h_plane = {(h, jt): h_plane_all[h][:, jt * P : (jt + 1) * P] for h, jt in pieces}
+        h_bf = [keep.tile([P, J, PACK], BF16, name=f"h_bf{h}", align_bytes=ALIGN) for h in range(HALVES)]
+        h_w = [keep.tile([P, J], U32, name=f"h_w{h}", align_bytes=ALIGN) for h in range(HALVES)]
+        h_plane = [keep.tile([P, J], U8, name=f"h_plane{h}", align_bytes=ALIGN) for h in range(HALVES)]
 
         def neighbour_pass(bank, u, g, start):
             h, jt = u
-            points = slice(jt * P, (jt + 1) * P)
-            first = (g % 2) * J + jt * P
+            picked = slice((g % 2) * J + jt * P, (g % 2) * J + (jt + 1) * P)
             nc.tensor.matmul_mx(
                 out=bank[:],
-                lhsT=nb_w[g][:, points].bitcast(FP8X4),
-                lhsT_scale=nb_plane[g // 2][:, first : first + P],
+                lhsT=nb_w[g // 2][:, picked].bitcast(FP8X4),
+                lhsT_scale=nb_plane[g // 2][:, picked],
                 rhs=w_w[:, h * BANK : (h + 1) * BANK].bitcast(FP8X4),
                 rhs_scale=w_plane[:].bitcast(U8)[:, h * BANK : (h + 1) * BANK],
                 start=start,
@@ -190,78 +180,73 @@ def tile_list_pnet_mix_none_kernel(
             )
 
         def neighbour(u, g):
-            if u == LAST:
-                bank = next_bank("scalar")
-                own_pass(bank, u, False)
-                neighbour_pass(bank, u, g, False)
-                nc.scalar.activation(in_sbuf(four_sums[:, g, :], u), from_bank(bank, u), ACT.Relu)
-                return
             bank = next_bank("scalar" if g == 0 else "vector")
             neighbour_pass(bank, u, g, True)
-            before = after = in_sbuf(pooled[u], u)
+            running = in_sbuf(pooled[u][:], u)
             if g == 0:
-                nc.scalar.activation(after, from_bank(bank, u), ACT.Copy)
+                nc.scalar.activation(running, from_bank(bank, u), ACT.Copy)
             else:
-                nc.vector.tensor_tensor(after, from_bank(bank, u), before, ALU.max)
+                nc.vector.tensor_tensor(running, from_bank(bank, u), running, ALU.max)
+
+        def neighbour_with_own_part(g):
+            bank = next_bank("scalar")
+            own_pass(bank, IN_EACH_SUM, False)
+            neighbour_pass(bank, IN_EACH_SUM, g, False)
+            nc.scalar.activation(in_sbuf(four_sums[:, g, :], IN_EACH_SUM), from_bank(bank, IN_EACH_SUM), ACT.Relu)
+
+        def last_neighbour_with_own_part(u):
+            bank = next_bank("scalar")
+            own_pass(bank, u, False)
+            neighbour_pass(bank, u, G - 1, False)
+            nc.scalar.activation(in_sbuf(last_sum[:], u), from_bank(bank, u), ACT.Relu)
+
+        def fold_last_sum(u):
+            nc.vector.tensor_tensor(summed[u][:], summed[u][:], last_sum[:], ALU.max)
 
         def own_part(u):
-            bank = next_bank("vector" if u in ADDED_ON_VECTOR else "scalar")
+            bank = next_bank("scalar")
             own_pass(bank, u, True)
-            if u in ADDED_ON_VECTOR:
-                nc.vector.tensor_tensor(in_sbuf(summed[u][:], u), from_bank(bank, u), in_sbuf(pooled[u], u), ALU.add)
-            else:
-                nc.scalar.activation(in_sbuf(own[u][:], u), from_bank(bank, u), ACT.Copy)
+            nc.scalar.activation(in_sbuf(own[u][:], u), from_bank(bank, u), ACT.Copy)
 
         def add_on_gpsimd(u):
-            nc.gpsimd.tensor_tensor(summed[u][:], pooled[u], own[u][:], ALU.add)
+            nc.gpsimd.tensor_tensor(summed[u][:], pooled[u][:], own[u][:], ALU.add)
 
         def turn(u):
-            rounded = h_bf[u]
-            if u in summed:
-                turned = next_bank("scalar")[:, : 2 * P].rearrange("p (a j) -> p a j", a=2)
-                pairs = summed[u][:].bitcast(F32)
-                for a in range(2):
-                    nc.tensor.transpose(turned[:, a, :], pairs[:, a * P : (a + 1) * P], ident[:])
-                if u == LAST:
-                    rounded_pairs = rounded[:].rearrange("p j t -> p (j t)").bitcast(F32)
-                    nc.scalar.copy(rounded_pairs.rearrange("p (j a) -> p j a", a=2), turned.rearrange("p a j -> p j a"))
-                elif u in RELU_ON_VECTOR:
-                    nc.vector.tensor_scalar(
-                        rounded[:].rearrange("p j (a e) -> p j a e", e=2),
-                        turned.bitcast(BF16).rearrange("p a (j e) -> p j a e", e=2),
-                        0.0,
-                        None,
-                        ALU.max,
-                    )
-                else:
-                    nc.scalar.activation(
-                        rounded[:].rearrange("p j (a e) -> p j a e", e=2),
-                        turned.bitcast(BF16).rearrange("p a (j e) -> p j a e", e=2),
-                        ACT.Relu,
-                    )
-            else:
+            h, jt = u
+            rounded = h_bf[h][:, jt * P : (jt + 1) * P, :]
+            if u not in AS_PAIRS:
                 turned = next_bank("scalar")[:].rearrange("p (t j) -> p t j", t=PACK)
                 for t in range(PACK):
                     cols = slice(t * P, (t + 1) * P)
-                    for term, start in ((pooled[u], True), (own[u][:], False)):
+                    for term, start in ((pooled[u], True), (own[u], False)):
                         nc.tensor.matmul(
                             turned[:, t, :], term[:, cols], ident[:], start=start, stop=not start, is_transpose=True
                         )
-                if u in RELU_ON_VECTOR:
-                    nc.vector.tensor_scalar(rounded[:], turned.rearrange("p t j -> p j t"), 0.0, None, ALU.max)
-                else:
-                    nc.scalar.activation(rounded[:], turned.rearrange("p t j -> p j t"), ACT.Relu)
+                nc.scalar.activation(rounded, turned.rearrange("p t j -> p j t"), ACT.Relu)
+                return
+            turned = next_bank("scalar")[:, : 2 * P].rearrange("p (a j) -> p a j", a=2)
+            pairs = summed[u][:].bitcast(F32)
+            for a in range(2):
+                nc.tensor.transpose(turned[:, a, :], pairs[:, a * P : (a + 1) * P], ident[:])
+            if u in (IN_EACH_SUM, LAST_SUM_APART):
+                rounded_pairs = rounded.rearrange("p j t -> p (j t)").bitcast(F32)
+                copy = nc.scalar.copy if u == IN_EACH_SUM else nc.vector.tensor_copy
+                copy(rounded_pairs.rearrange("p (j a) -> p j a", a=2), turned.rearrange("p a j -> p j a"))
+                return
+            values = turned.bitcast(BF16).rearrange("p a (j e) -> p j a e", e=2)
+            in_order = rounded.rearrange("p j (a e) -> p j a e", e=2)
+            nc.scalar.activation(in_order, values, ACT.Relu)
 
-        def quantise_h(h, jt, count):
-            quantise(h_w_all[h], h_plane_all[h], h_bf_all[h], slice(jt * P, (jt + count) * P))
+        def quantise_h(h, first_tile, tiles):
+            quantise(h_w[h], h_plane[h], h_bf[h], slice(first_tile * P, (first_tile + tiles) * P))
 
-        def result_passes(y, nt, jt):
+        def result_passes(y, nt, points):
             nc.tensor.matmul_mx(
                 out=y,
                 lhsT=wd8_w[:, nt * P : (nt + 1) * P].bitcast(FP8X4),
                 lhsT_scale=wd8_plane[:].bitcast(U8)[:, nt * P : (nt + 1) * P],
-                rhs=h_w[0, jt][:].bitcast(FP8X4),
-                rhs_scale=h_plane[0, jt][:],
+                rhs=h_w[0][:, points].bitcast(FP8X4),
+                rhs_scale=h_plane[0][:, points],
                 start=True,
                 stop=False,
             )
@@ -269,73 +254,77 @@ def tile_list_pnet_mix_none_kernel(
                 out=y,
                 lhsT=wd4_w[:, 2 * nt * P : 2 * (nt + 1) * P].bitcast(FP4X4),
                 lhsT_scale=wd4_plane[:].bitcast(U8)[:, nt * P : (nt + 1) * P],
-                rhs=h_w[1, jt][:].bitcast(FP8X4),
-                rhs_scale=h_plane[1, jt][:],
+                rhs=h_w[1][:, points].bitcast(FP8X4),
+                rhs_scale=h_plane[1][:, points],
                 start=False,
                 stop=True,
             )
 
-        def second_layer(jt, reader):
+        def second_layer(jt):
             points = slice(jt * P, (jt + 1) * P)
             y_sb = keep.tile([P, N // P, P], F32, name=f"y_sb{jt}")
-            if reader == "both":
-                upper = next_bank("vector")[:, :P]
-                result_passes(upper, 0, jt)
-                lower = next_bank("vector")[:, :P]
-                result_passes(lower, 1, jt)
-                nc.vector.tensor_copy(y_sb[:, 0, :], upper)
-                nc.sync.dma_start(out=out[:P, points], in_=y_sb[:, 0, :])
-                nc.scalar.activation(y_sb[:, 1, :], lower, ACT.Copy)
-                nc.scalar.dma_start(out=out[P:, points], in_=y_sb[:, 1, :])
-                return
-            y = next_bank("vector")[:, :N].rearrange("n (nt j) -> n nt j", j=P)
-            for nt in range(N // P):
-                result_passes(y[:, nt, :], nt, jt)
-            if reader == "scalar":
+            if jt < POINT_TILES - 1:
+                y = next_bank("vector")[:, :N].rearrange("n (nt j) -> n nt j", j=P)
+                for nt in range(N // P):
+                    result_passes(y[:, nt, :], nt, points)
                 nc.scalar.activation(y_sb[:], y, ACT.Copy)
-            else:
-                nc.vector.tensor_copy(y_sb[:], y)
-            nc.sync.dma_start(out=out[:, points].rearrange("(nt n) j -> n nt j", n=P), in_=y_sb[:])
+                nc.sync.dma_start(out=out[:, points].rearrange("(nt n) j -> n nt j", n=P), in_=y_sb[:])
+                return
+            upper = next_bank("vector")[:, :P]
+            result_passes(upper, 0, points)
+            lower = next_bank("vector")[:, :P]
+            result_passes(lower, 1, points)
+            nc.vector.tensor_copy(y_sb[:, 0, :], upper)
+            nc.sync.dma_start(out=out[:P, points], in_=y_sb[:, 0, :])
+            nc.scalar.activation(y_sb[:, 1, :], lower, ACT.Copy)
+            nc.scalar.dma_start(out=out[P:, points], in_=y_sb[:, 1, :])
 
         whole = slice(0, BANK)
-        for pair in range(G // 2):
-            gather_scales(pair)
+        for pair in range(PAIRS):
+            nc.vector.tensor_copy(nb_plane[pair][:], tab_plane[:].bitcast(U8).indirect(entries[pair]))
         round_rows(c_bf, c_raw, whole)
         quantise(c_w, c_plane, c_bf, whole)
-        round_rows(wc_bf[0], wc_raw[0], slice(0, BANK - 0))
-        if 0:
-            round_rows_on_vector(wc_bf[0], wc_raw[0], slice(BANK - 0, BANK))
-        quantise(wc_w[0], wc_plane[0], wc_bf[0], whole)
-        for g in range(G // 2):
-            gather_words(g)
-        maxima = sorted(((u, g) for u in ranked for g in range(1, G)), key=lambda ug: 3 * ranked.index(ug[0]) + 2 * ug[1])
-        after = {u: place + 1 for place, (u, g) in enumerate(maxima)}
+        round_rows(wc_bf, wc_raw[0], whole)
+        quantise(wc_w[0], wc_plane[0], wc_bf, whole)
+        for pair in range(PAIRS):
+            nc.vector.tensor_copy(nb_w[pair][:], tab_w[:].indirect(entries[pair]))
+
+        first_at = {u: 3 * rank - FIRST_LEAD for rank, u in enumerate(RANKED)}
+        for u in RANKED:
+            if first_at[u] < 0:
+                neighbour(u, 0)
+        round_rows_on_gpsimd(wc_bf, wc_raw[1], slice(0, GPSIMD_COLUMNS))
+        round_rows(wc_bf, wc_raw[1], slice(GPSIMD_COLUMNS, BANK))
+
+        maxima = sorted(
+            ((u, g) for u in RANKED for g in range(1, G) if (u, g) != (LAST_SUM_APART, G - 1)),
+            key=lambda ug: 3 * RANKED.index(ug[0]) + 2 * ug[1],
+        )
+        last = {u: number for number, (u, g) in enumerate(maxima)}
         end = len(maxima)
-        for u in ranked[:3]:
-            neighbour(u, 0)
-        round_rows_on_gpsimd(wc_bf[1], wc_raw[1], slice(0, 256))
-        round_rows(wc_bf[1], wc_raw[1], slice(256, BANK))
-        steps = [(1, quantise, (wc_w[1], wc_plane[1], wc_bf[1], whole))]
-        steps.extend((3 * rank - 5, neighbour, (u, 0)) for rank, u in enumerate(ranked) if rank >= 3)
-        steps.extend((after[u], own_part, (u,)) for u in ranked)
-        steps.extend((5 + 5 * g, neighbour, (LAST, g)) for g in range(G))
-        steps.extend((after[u], add_on_gpsimd, (u,)) for u in ADDED_ON_GPSIMD)
-        turn_at = {u: after[u] - 1 + (9 if u in ADDED_ON_GPSIMD else 5) for u in ranked}
-        steps.extend((turn_at[u], turn, (u,)) for u in ranked if turn_at[u] <= end)
+        turn_at = {u: last[u] + (TURN_LAG_GPSIMD if u in ON_GPSIMD else TURN_LAG) for u in RANKED}
+        steps = [(1, quantise, (wc_w[1], wc_plane[1], wc_bf, whole))]
+        steps.extend((first_at[u], neighbour, (u, 0)) for u in RANKED if first_at[u] >= 0)
+        steps.extend((last[u] + 1, own_part, (u,)) for u in RANKED)
+        steps.extend((EACH_SUM_STEP * (g + 1), neighbour_with_own_part, (g,)) for g in range(G))
+        steps.extend((last[u] + 1, add_on_gpsimd, (u,)) for u in ON_GPSIMD)
+        steps.append((last[LAST_SUM_APART] + LAST_SUM_LAG, last_neighbour_with_own_part, (LAST_SUM_APART,)))
+        steps.append((end - 1, fold_last_sum, (LAST_SUM_APART,)))
+        steps.extend((turn_at[u], turn, (u,)) for u in RANKED if turn_at[u] <= end)
         steps.append((end - 1, quantise_h, (0, 0, 2)))
-        steps.extend((place, neighbour, ug) for place, ug in enumerate(maxima))
-        for place, call, arguments in sorted(steps, key=lambda step: step[0]):
+        steps.extend((number, neighbour, ug) for number, ug in enumerate(maxima))
+        for number, call, arguments in sorted(steps, key=lambda step: step[0]):
             call(*arguments)
+
         nc.vector.tensor_tensor(two_sums[:], four_sums[:, :2, :], four_sums[:, 2:, :], ALU.max)
-        nc.vector.tensor_tensor(summed[LAST][:], two_sums[:, 0, :], two_sums[:, 1, :], ALU.max)
-        late = sorted((u for u in ranked if turn_at[u] > end), key=turn_at.get)
-        for u in late:
+        nc.vector.tensor_tensor(summed[IN_EACH_SUM][:], two_sums[:, 0, :], two_sums[:, 1, :], ALU.max)
+        for u in sorted((u for u in RANKED if turn_at[u] > end), key=turn_at.get):
             turn(u)
         quantise_h(1, 0, 1)
-        second_layer(0, "scalar")
-        turn(LAST)
+        second_layer(0)
+        turn(IN_EACH_SUM)
         for jt in range(1, POINT_TILES):
             if jt >= 2:
                 quantise_h(0, jt, 1)
             quantise_h(1, jt, 1)
-            second_layer(jt, "both" if jt >= 3 else "scalar")
+            second_layer(jt)

@@ -27,12 +27,17 @@ PAIR_COLS = 2 * J // 16
 ALIGN = 256
 BANKS_A_SET = 4
 
-RANKED = ((0, 0), (0, 1), (1, 0), (1, 1), (0, 2), (1, 2), (1, 3))
+RANKED = ((0, 0), (0, 1), (0, 2), (1, 0), (1, 1), (1, 2), (1, 3))
 IN_EACH_SUM = (0, 3)
 ON_GPSIMD = RANKED[1:-2]
 LAST_SUM_APART = ON_GPSIMD[-1]
-AS_PAIRS = (IN_EACH_SUM, *ON_GPSIMD)
-GPSIMD_COLUMNS = 256
+ADDED_ON_VECTOR = ()
+AS_PAIRS = (IN_EACH_SUM, *ON_GPSIMD, *ADDED_ON_VECTOR)
+GPSIMD_COLUMNS = 320
+GPSIMD_FIRST = 128
+GATED_FIRST = ((RANKED[3], 1), (RANKED[0], 2), (RANKED[1], 2), (RANKED[2], 2))
+ON_VECTOR = ()
+GATED = ((RANKED[2], 3), (RANKED[3], 2), (RANKED[4], 1))
 
 FIRST_LEAD = 8
 EACH_SUM_STEP = 5
@@ -59,6 +64,7 @@ def tile_list_pnet_mix_none_kernel(
     nc = tc.nc
     with ExitStack() as ctx:
         keep = ctx.enter_context(tc.tile_pool(name="keep", bufs=1))
+        shared = ctx.enter_context(tc.tile_pool(name="shared", bufs=1))
         psum = ctx.enter_context(tc.psum_pool(name="psum", bufs=1))
 
         banks = [psum.tile([P, BANK], F32, name=f"bank{b}") for b in range(2 * BANKS_A_SET)]
@@ -80,7 +86,7 @@ def tile_list_pnet_mix_none_kernel(
         wd8_w = keep.tile([P, N], U32, name="wd8_w", align_bytes=ALIGN)
         wd4_w = keep.tile([P, 2 * N], U8, name="wd4_w", align_bytes=ALIGN)
         c_raw = keep.tile([P, PACK, J], F32, name="c_raw")
-        wc_raw = [keep.tile([P, PACK, BANK], F32, name=f"wc_raw{h}") for h in range(HALVES)]
+        wc_raw = [shared.tile([P, PACK, BANK], F32, name=f"wc_raw{h}", offset=8192 * h) for h in range(HALVES)]
         ident = keep.tile([P, P], F32, name="ident")
 
         nc.vector.memset(tab_plane[:, : T // 8], 0)
@@ -95,16 +101,19 @@ def tile_list_pnet_mix_none_kernel(
         load_plane(nc, tab_plane, tab_scales[0])
         load_words(nc, tab_w, tab_words[0].rearrange("p t i -> p (t i)"))
         nc.sync.dma_start(out=c_raw[:], in_=c.rearrange("(p i) j -> p i j", i=PACK))
-        nc.sync.dma_start(out=wc_raw[0][:], in_=wc_rows[:, :, :BANK])
-        load_words(nc, w_w, w_words[0].rearrange("p r i -> p (r i)"))
         load_plane(nc, w_plane, w_scales[0])
+        w_bytes = w_words[0].rearrange("p r i -> p (r i)")
+        load_words(nc, w_w, w_bytes)
+        nc.sync.dma_start(out=wc_raw[0][:], in_=wc_rows[:, :, :BANK])
         nc.sync.dma_start(out=wc_raw[1][:], in_=wc_rows[:, :, BANK:])
         load_words(nc, wd4_w, wd4_words[0])
         load_words(nc, wd8_w, wd8_words[0].rearrange("p n i -> p (n i)"))
         load_plane(nc, wd4_plane, wd4_scales[0])
         load_plane(nc, wd8_plane, wd8_scales[0])
 
-        nb_w = [keep.tile([P, 2 * J], U32, name=f"nb_w{pair}", align_bytes=ALIGN) for pair in range(PAIRS)]
+        nb_first = [keep.tile([P, J], U32, name=f"nb_first{g}", align_bytes=ALIGN) for g in range(2)]
+        nb_last = keep.tile([P, 2 * J], U32, name="nb_last", align_bytes=ALIGN)
+        nb_w = [nb_first[0][:], nb_first[1][:], nb_last[:, :J], nb_last[:, J:]]
         nb_plane = [keep.tile([P, 2 * J], U8, name=f"nb_plane{pair}", align_bytes=ALIGN) for pair in range(PAIRS)]
         entries = [offsets[:, pair * PAIR_COLS : (pair + 1) * PAIR_COLS] for pair in range(PAIRS)]
 
@@ -112,26 +121,32 @@ def tile_list_pnet_mix_none_kernel(
         c_plane = keep.tile([P, J], U8, name="c_plane", align_bytes=ALIGN)
         wc_w = [keep.tile([P, BANK], U32, name=f"wc_w{h}", align_bytes=ALIGN) for h in range(HALVES)]
         wc_plane = [keep.tile([P, BANK], U8, name=f"wc_plane{h}", align_bytes=ALIGN) for h in range(HALVES)]
-        wc_bf = keep.tile([P, BANK, PACK], BF16, name="wc_bf", align_bytes=ALIGN)
-        c_bf = keep.tile([P, J, PACK], BF16, name="c_bf", align_bytes=ALIGN)
+        rounded_first = shared.tile([P, (J + BANK) * PACK], BF16, name="rounded_first", align_bytes=ALIGN, offset=16384)
+        wc_bf = [rounded_first[:, (J - GPSIMD_FIRST) * PACK : (J - GPSIMD_FIRST + BANK) * PACK], shared.tile([P, BANK * PACK], BF16, name="wc_bf1", align_bytes=ALIGN, offset=16384)[:]]
+        c_bf = rounded_first[:, : J * PACK]
 
         def round_rows(rounded, raw, cols):
             nc.scalar.activation(
-                rounded[:, cols, :].rearrange("p (a b) i -> p a i b", b=4),
+                rounded[:, PACK * cols.start : PACK * cols.stop].rearrange("p (a b i) -> p a i b", b=4, i=PACK),
                 raw[:, :, cols].rearrange("p i (a b) -> p a i b", b=4),
                 ACT.Copy,
             )
 
         def round_rows_on_gpsimd(rounded, raw, cols):
             nc.gpsimd.tensor_scalar(
-                rounded[:, cols, :], raw[:, :, cols].rearrange("p i a -> p a i"), 1.0, 0.0, ALU.mult, ALU.add
+                rounded[:, PACK * cols.start : PACK * cols.stop].rearrange("p (a i) -> p a i", i=PACK),
+                raw[:, :, cols].rearrange("p i a -> p a i"),
+                1.0,
+                0.0,
+                ALU.mult,
+                ALU.add,
             )
 
         def quantise(words, plane, rounded, cols):
             nc.vector.quantize_mx(
                 out=words[:, cols].bitcast(FP8X4),
                 scales=plane[:, cols],
-                in_=rounded[:, cols, :].rearrange("p a i -> p (a i)"),
+                in_=rounded[:, PACK * cols.start : PACK * cols.stop],
             )
 
         def from_bank(bank, u):
@@ -145,13 +160,28 @@ def tile_list_pnet_mix_none_kernel(
             return columns.rearrange("j (t b q) -> j b t q", q=4, t=PACK)
 
         pooled = {u: keep.tile([P, BANK], F32, name=f"pooled{u[0]}{u[1]}") for u in RANKED}
-        own = {u: keep.tile([P, BANK], F32, name=f"own{u[0]}{u[1]}") for u in RANKED}
-        summed = {u: keep.tile([P, BANK], BF16, name=f"summed{u[0]}{u[1]}") for u in AS_PAIRS}
+        moves = {ug: n for n, ug in enumerate(GATED_FIRST)}
+        moves.update({ug: 4 + n for n, ug in enumerate(GATED)})
+        running = {(u, 0): pooled[u] for u in RANKED}
+        for u in RANKED:
+            for g in range(1, G):
+                if (u, g) in moves:
+                    running[u, g] = shared.tile([P, BANK], F32, name=f"moved{u[0]}{u[1]}{g}", offset=2048 * moves[u, g])
+                else:
+                    running[u, g] = running[u, g - 1]
+        later = {u: running[u, G - 1] for u in RANKED}
+        own = {u: keep.tile([P, BANK], F32, name=f"own{u[0]}{u[1]}") for u in RANKED if u != LAST_SUM_APART}
+        own[LAST_SUM_APART] = shared.tile([P, BANK], F32, name="own_b", align_bytes=ALIGN, offset=24576)
+        summed = {u: keep.tile([P, BANK], BF16, name=f"summed{u[0]}{u[1]}") for u in AS_PAIRS if u != ON_GPSIMD[0]}
+        summed[ON_GPSIMD[0]] = shared.tile([P, BANK], BF16, name="summed_first", align_bytes=ALIGN, offset=16384)
         last_sum = keep.tile([P, BANK], BF16, name="last_sum")
         four_sums = keep.tile([P, G, BANK], BF16, name="four_sums")
         two_sums = keep.tile([P, G // 2, BANK], BF16, name="two_sums")
-        h_bf = [keep.tile([P, J, PACK], BF16, name=f"h_bf{h}", align_bytes=ALIGN) for h in range(HALVES)]
-        h_w = [keep.tile([P, J], U32, name=f"h_w{h}", align_bytes=ALIGN) for h in range(HALVES)]
+        h_first = keep.tile([P, 2 * P * PACK], BF16, name="h_first", align_bytes=ALIGN)
+        h_bf = {(0, 0): h_first[:, : P * PACK], (0, 1): h_first[:, P * PACK :]}
+        for u in (*RANKED[2:], IN_EACH_SUM):
+            h_bf[u] = keep.tile([P, P * PACK], BF16, name=f"h_bf{u[0]}{u[1]}", align_bytes=ALIGN)[:]
+        h_w = [shared.tile([P, J], U32, name="h_w0", align_bytes=ALIGN, offset=24576), keep.tile([P, J], U32, name="h_w1", align_bytes=ALIGN)]
         h_plane = [keep.tile([P, J], U8, name=f"h_plane{h}", align_bytes=ALIGN) for h in range(HALVES)]
 
         def neighbour_pass(bank, u, g, start):
@@ -159,7 +189,7 @@ def tile_list_pnet_mix_none_kernel(
             picked = slice((g % 2) * J + jt * P, (g % 2) * J + (jt + 1) * P)
             nc.tensor.matmul_mx(
                 out=bank[:],
-                lhsT=nb_w[g // 2][:, picked].bitcast(FP8X4),
+                lhsT=nb_w[g][:, jt * P : (jt + 1) * P].bitcast(FP8X4),
                 lhsT_scale=nb_plane[g // 2][:, picked],
                 rhs=w_w[:, h * BANK : (h + 1) * BANK].bitcast(FP8X4),
                 rhs_scale=w_plane[:].bitcast(U8)[:, h * BANK : (h + 1) * BANK],
@@ -179,14 +209,20 @@ def tile_list_pnet_mix_none_kernel(
                 stop=stop,
             )
 
-        def neighbour(u, g):
+        held = []
+
+        def neighbour(u, g, later_on=False):
             bank = next_bank("scalar" if g == 0 else "vector")
             neighbour_pass(bank, u, g, True)
-            running = in_sbuf(pooled[u][:], u)
             if g == 0:
-                nc.scalar.activation(running, from_bank(bank, u), ACT.Copy)
+                nc.scalar.activation(in_sbuf(pooled[u][:], u), from_bank(bank, u), ACT.Copy)
             else:
-                nc.vector.tensor_tensor(running, from_bank(bank, u), running, ALU.max)
+                before = in_sbuf(running[u, g - 1][:], u)
+                after = in_sbuf(running[u, g][:], u)
+                if later_on:
+                    held.append(lambda: nc.vector.tensor_tensor(after, from_bank(bank, u), before, ALU.max))
+                else:
+                    nc.vector.tensor_tensor(after, from_bank(bank, u), before, ALU.max)
 
         def neighbour_with_own_part(g):
             bank = next_bank("scalar")
@@ -208,17 +244,22 @@ def tile_list_pnet_mix_none_kernel(
             own_pass(bank, u, True)
             nc.scalar.activation(in_sbuf(own[u][:], u), from_bank(bank, u), ACT.Copy)
 
+        def add_on_vector(u):
+            bank = next_bank("vector")
+            own_pass(bank, u, True)
+            held.append(lambda: nc.vector.tensor_tensor(in_sbuf(summed[u][:], u), from_bank(bank, u), in_sbuf(later[u][:], u), ALU.add))
+
         def add_on_gpsimd(u):
-            nc.gpsimd.tensor_tensor(summed[u][:], pooled[u][:], own[u][:], ALU.add)
+            nc.gpsimd.tensor_tensor(summed[u][:], later[u][:], own[u][:], ALU.add)
 
         def turn(u):
             h, jt = u
-            rounded = h_bf[h][:, jt * P : (jt + 1) * P, :]
+            rounded = h_bf[u].rearrange("p (j t) -> p j t", t=PACK)
             if u not in AS_PAIRS:
                 turned = next_bank("scalar")[:].rearrange("p (t j) -> p t j", t=PACK)
                 for t in range(PACK):
                     cols = slice(t * P, (t + 1) * P)
-                    for term, start in ((pooled[u], True), (own[u], False)):
+                    for term, start in ((later[u], True), (own[u], False)):
                         nc.tensor.matmul(
                             turned[:, t, :], term[:, cols], ident[:], start=start, stop=not start, is_transpose=True
                         )
@@ -230,7 +271,7 @@ def tile_list_pnet_mix_none_kernel(
                 nc.tensor.transpose(turned[:, a, :], pairs[:, a * P : (a + 1) * P], ident[:])
             if u in (IN_EACH_SUM, LAST_SUM_APART):
                 rounded_pairs = rounded.rearrange("p j t -> p (j t)").bitcast(F32)
-                copy = nc.scalar.copy if u == IN_EACH_SUM else nc.vector.tensor_copy
+                copy = nc.vector.tensor_copy if u in ON_VECTOR else nc.scalar.copy
                 copy(rounded_pairs.rearrange("p (j a) -> p j a", a=2), turned.rearrange("p a j -> p j a"))
                 return
             values = turned.bitcast(BF16).rearrange("p a (j e) -> p j a e", e=2)
@@ -238,7 +279,12 @@ def tile_list_pnet_mix_none_kernel(
             nc.scalar.activation(in_order, values, ACT.Relu)
 
         def quantise_h(h, first_tile, tiles):
-            quantise(h_w[h], h_plane[h], h_bf[h], slice(first_tile * P, (first_tile + tiles) * P))
+            cols = slice(first_tile * P, (first_tile + tiles) * P)
+            nc.vector.quantize_mx(
+                out=h_w[h][:, cols].bitcast(FP8X4),
+                scales=h_plane[h][:, cols],
+                in_=h_first[:] if tiles == 2 else h_bf[h, first_tile],
+            )
 
         def result_passes(y, nt, points):
             nc.tensor.matmul_mx(
@@ -282,49 +328,81 @@ def tile_list_pnet_mix_none_kernel(
         whole = slice(0, BANK)
         for pair in range(PAIRS):
             nc.vector.tensor_copy(nb_plane[pair][:], tab_plane[:].bitcast(U8).indirect(entries[pair]))
+        for g in range(2):
+            nc.vector.tensor_copy(nb_w[g], tab_w[:].indirect(entries[0][:, g * PAIR_COLS // 2 : (g + 1) * PAIR_COLS // 2]))
+        nc.vector.tensor_copy(nb_last[:], tab_w[:].indirect(entries[1]))
         round_rows(c_bf, c_raw, whole)
         quantise(c_w, c_plane, c_bf, whole)
-        round_rows(wc_bf, wc_raw[0], whole)
-        quantise(wc_w[0], wc_plane[0], wc_bf, whole)
-        for pair in range(PAIRS):
-            nc.vector.tensor_copy(nb_w[pair][:], tab_w[:].indirect(entries[pair]))
-
-        first_at = {u: 3 * rank - FIRST_LEAD for rank, u in enumerate(RANKED)}
-        for u in RANKED:
-            if first_at[u] < 0:
-                neighbour(u, 0)
-        round_rows_on_gpsimd(wc_bf, wc_raw[1], slice(0, GPSIMD_COLUMNS))
-        round_rows(wc_bf, wc_raw[1], slice(GPSIMD_COLUMNS, BANK))
-
-        maxima = sorted(
-            ((u, g) for u in RANKED for g in range(1, G) if (u, g) != (LAST_SUM_APART, G - 1)),
-            key=lambda ug: 3 * RANKED.index(ug[0]) + 2 * ug[1],
-        )
-        last = {u: number for number, (u, g) in enumerate(maxima)}
-        end = len(maxima)
-        turn_at = {u: last[u] + (TURN_LAG_GPSIMD if u in ON_GPSIMD else TURN_LAG) for u in RANKED}
-        steps = [(1, quantise, (wc_w[1], wc_plane[1], wc_bf, whole))]
-        steps.extend((first_at[u], neighbour, (u, 0)) for u in RANKED if first_at[u] >= 0)
-        steps.extend((last[u] + 1, own_part, (u,)) for u in RANKED)
-        steps.extend((EACH_SUM_STEP * (g + 1), neighbour_with_own_part, (g,)) for g in range(G))
-        steps.extend((last[u] + 1, add_on_gpsimd, (u,)) for u in ON_GPSIMD)
-        steps.append((last[LAST_SUM_APART] + LAST_SUM_LAG, last_neighbour_with_own_part, (LAST_SUM_APART,)))
-        steps.append((end - 1, fold_last_sum, (LAST_SUM_APART,)))
-        steps.extend((turn_at[u], turn, (u,)) for u in RANKED if turn_at[u] <= end)
-        steps.append((end - 1, quantise_h, (0, 0, 2)))
-        steps.extend((number, neighbour, ug) for number, ug in enumerate(maxima))
-        for number, call, arguments in sorted(steps, key=lambda step: step[0]):
-            call(*arguments)
-
+        A, B, C, D, E, F, H = RANKED
+        neighbour(A, 0)
+        neighbour(B, 0)
+        neighbour(C, 0)
+        round_rows_on_gpsimd(wc_bf[0], wc_raw[0], slice(0, GPSIMD_FIRST))
+        round_rows(wc_bf[0], wc_raw[0], slice(GPSIMD_FIRST, BANK))
+        neighbour(D, 0)
+        neighbour(A, 1)
+        neighbour(B, 1)
+        neighbour(C, 1)
+        quantise(wc_w[0], wc_plane[0], wc_bf[0], whole)
+        neighbour(D, 1)
+        neighbour(E, 0)
+        neighbour(F, 0)
+        neighbour(H, 0)
+        round_rows_on_gpsimd(wc_bf[1], wc_raw[1], slice(0, GPSIMD_COLUMNS))
+        own_part(A)
+        neighbour(A, 2)
+        own_part(B)
+        neighbour(B, 2)
+        round_rows(wc_bf[1], wc_raw[1], slice(GPSIMD_COLUMNS, BANK))
+        neighbour(A, 3)
+        neighbour_with_own_part(0)
+        neighbour(B, 3)
+        neighbour_with_own_part(1)
+        neighbour(C, 2)
+        turn(A)
+        quantise(wc_w[1], wc_plane[1], wc_bf[1], whole)
+        add_on_gpsimd(B)
+        neighbour(C, 3)
+        own_part(C)
+        add_on_gpsimd(C)
+        neighbour(D, 2)
+        neighbour(E, 1)
+        own_part(D)
+        neighbour(D, 3)
+        add_on_gpsimd(D)
+        own_part(E)
+        neighbour(E, 2)
+        add_on_gpsimd(E)
+        neighbour(F, 1)
+        neighbour_with_own_part(2)
+        neighbour(H, 1)
+        own_part(F)
+        neighbour(F, 2)
+        neighbour_with_own_part(3)
+        neighbour(H, 2)
+        last_neighbour_with_own_part(LAST_SUM_APART)
+        neighbour(F, 3)
+        own_part(H)
+        neighbour(H, 3, later_on=True)
+        turn(B)
+        turn(C)
+        turn(D)
+        fold_last_sum(LAST_SUM_APART)
+        turn(F)
+        held.pop(0)()
+        turn(E)
         nc.vector.tensor_tensor(two_sums[:], four_sums[:, :2, :], four_sums[:, 2:, :], ALU.max)
+        turn(H)
+        quantise_h(0, 0, 2)
         nc.vector.tensor_tensor(summed[IN_EACH_SUM][:], two_sums[:, 0, :], two_sums[:, 1, :], ALU.max)
-        for u in sorted((u for u in RANKED if turn_at[u] > end), key=turn_at.get):
-            turn(u)
         quantise_h(1, 0, 1)
-        second_layer(0)
         turn(IN_EACH_SUM)
-        for jt in range(1, POINT_TILES):
-            if jt >= 2:
-                quantise_h(0, jt, 1)
-            quantise_h(1, jt, 1)
-            second_layer(jt)
+        second_layer(0)
+        quantise_h(0, 2, 1)
+        quantise_h(1, 1, 1)
+        second_layer(1)
+        quantise_h(1, 2, 1)
+        second_layer(2)
+        quantise_h(1, 3, 1)
+        quantise_h(0, 3, 1)
+        second_layer(3)

@@ -32,11 +32,12 @@ IN_EACH_SUM = (0, 3)
 ON_GPSIMD = RANKED[1:-2]
 LAST_SUM_APART = ON_GPSIMD[-1]
 ADDED_ON_VECTOR = ()
+Y_ON_VECTOR = ()
 AS_PAIRS = (IN_EACH_SUM, *ON_GPSIMD, *ADDED_ON_VECTOR)
-GPSIMD_COLUMNS = 320
+GPSIMD_COLUMNS = 256
 GPSIMD_FIRST = 128
 GATED_FIRST = ((RANKED[3], 1), (RANKED[0], 2), (RANKED[1], 2), (RANKED[2], 2))
-ON_VECTOR = ()
+ON_VECTOR = (IN_EACH_SUM,)
 GATED = ((RANKED[2], 3), (RANKED[3], 2), (RANKED[4], 1))
 
 FIRST_LEAD = 8
@@ -170,18 +171,17 @@ def tile_list_pnet_mix_none_kernel(
                 else:
                     running[u, g] = running[u, g - 1]
         later = {u: running[u, G - 1] for u in RANKED}
-        own = {u: keep.tile([P, BANK], F32, name=f"own{u[0]}{u[1]}") for u in RANKED if u != LAST_SUM_APART}
-        own[LAST_SUM_APART] = shared.tile([P, BANK], F32, name="own_b", align_bytes=ALIGN, offset=24576)
+        own = {u: keep.tile([P, BANK], F32, name=f"own{u[0]}{u[1]}") for u in RANKED}
         summed = {u: keep.tile([P, BANK], BF16, name=f"summed{u[0]}{u[1]}") for u in AS_PAIRS if u != ON_GPSIMD[0]}
         summed[ON_GPSIMD[0]] = shared.tile([P, BANK], BF16, name="summed_first", align_bytes=ALIGN, offset=16384)
-        last_sum = keep.tile([P, BANK], BF16, name="last_sum")
+        last_sum = shared.tile([P, BANK], BF16, name="last_sum", align_bytes=ALIGN, offset=24576 + 1536)
         four_sums = keep.tile([P, G, BANK], BF16, name="four_sums")
         two_sums = keep.tile([P, G // 2, BANK], BF16, name="two_sums")
         h_first = keep.tile([P, 2 * P * PACK], BF16, name="h_first", align_bytes=ALIGN)
         h_bf = {(0, 0): h_first[:, : P * PACK], (0, 1): h_first[:, P * PACK :]}
         for u in (*RANKED[2:], IN_EACH_SUM):
             h_bf[u] = keep.tile([P, P * PACK], BF16, name=f"h_bf{u[0]}{u[1]}", align_bytes=ALIGN)[:]
-        h_w = [shared.tile([P, J], U32, name="h_w0", align_bytes=ALIGN, offset=24576), keep.tile([P, J], U32, name="h_w1", align_bytes=ALIGN)]
+        h_w = [shared.tile([P, J], U32, name=f"h_w{h}", align_bytes=ALIGN, offset=24576 + 2048 * h) for h in range(HALVES)]
         h_plane = [keep.tile([P, J], U8, name=f"h_plane{h}", align_bytes=ALIGN) for h in range(HALVES)]
 
         def neighbour_pass(bank, u, g, start):
@@ -252,9 +252,27 @@ def tile_list_pnet_mix_none_kernel(
         def add_on_gpsimd(u):
             nc.gpsimd.tensor_tensor(summed[u][:], later[u][:], own[u][:], ALU.add)
 
+        begun = {}
+
+        def begin_turn(u):
+            turned = next_bank("scalar")[:].rearrange("p (t j) -> p t j", t=PACK)
+            for t in range(PACK):
+                nc.tensor.matmul(
+                    turned[:, t, :], own[u][:, t * P : (t + 1) * P], ident[:], start=t == 0, stop=False, is_transpose=True
+                )
+            begun[u] = turned
+
         def turn(u):
             h, jt = u
             rounded = h_bf[u].rearrange("p (j t) -> p j t", t=PACK)
+            if u in begun:
+                turned = begun[u]
+                for t in range(PACK):
+                    nc.tensor.matmul(
+                        turned[:, t, :], later[u][:, t * P : (t + 1) * P], ident[:], start=False, stop=t == PACK - 1, is_transpose=True
+                    )
+                nc.scalar.activation(rounded, turned.rearrange("p t j -> p j t"), ACT.Relu)
+                return
             if u not in AS_PAIRS:
                 turned = next_bank("scalar")[:].rearrange("p (t j) -> p t j", t=PACK)
                 for t in range(PACK):
@@ -313,7 +331,10 @@ def tile_list_pnet_mix_none_kernel(
                 y = next_bank("vector")[:, :N].rearrange("n (nt j) -> n nt j", j=P)
                 for nt in range(N // P):
                     result_passes(y[:, nt, :], nt, points)
-                nc.scalar.activation(y_sb[:], y, ACT.Copy)
+                if jt in Y_ON_VECTOR:
+                    nc.vector.tensor_copy(y_sb[:], y)
+                else:
+                    nc.scalar.activation(y_sb[:], y, ACT.Copy)
                 nc.sync.dma_start(out=out[:, points].rearrange("(nt n) j -> n nt j", n=P), in_=y_sb[:])
                 return
             upper = next_bank("vector")[:, :P]
@@ -376,33 +397,34 @@ def tile_list_pnet_mix_none_kernel(
         neighbour(F, 1)
         neighbour_with_own_part(2)
         neighbour(H, 1)
-        own_part(F)
+        turn(B)
+        turn(C)
         neighbour(F, 2)
-        neighbour_with_own_part(3)
+        own_part(F)
         neighbour(H, 2)
         last_neighbour_with_own_part(LAST_SUM_APART)
         neighbour(F, 3)
-        own_part(H)
+        neighbour_with_own_part(3)
         neighbour(H, 3, later_on=True)
-        turn(B)
-        turn(C)
+        own_part(H)
         turn(D)
         fold_last_sum(LAST_SUM_APART)
         turn(F)
+        begin_turn(H)
+        nc.vector.tensor_tensor(two_sums[:], four_sums[:, :2, :], four_sums[:, 2:, :], ALU.max)
         held.pop(0)()
         turn(E)
-        nc.vector.tensor_tensor(two_sums[:], four_sums[:, :2, :], four_sums[:, 2:, :], ALU.max)
-        turn(H)
-        quantise_h(0, 0, 2)
         nc.vector.tensor_tensor(summed[IN_EACH_SUM][:], two_sums[:, 0, :], two_sums[:, 1, :], ALU.max)
-        quantise_h(1, 0, 1)
+        turn(H)
         turn(IN_EACH_SUM)
+        quantise_h(0, 0, 2)
+        quantise_h(1, 0, 1)
         second_layer(0)
         quantise_h(0, 2, 1)
         quantise_h(1, 1, 1)
         second_layer(1)
         quantise_h(1, 2, 1)
         second_layer(2)
-        quantise_h(1, 3, 1)
         quantise_h(0, 3, 1)
+        quantise_h(1, 3, 1)
         second_layer(3)

@@ -90,15 +90,16 @@ def tile_list_pnet_mix_none_kernel(
         wc_raw = [shared.tile([P, PACK, BANK], F32, name=f"wc_raw{h}", offset=8192 * h) for h in range(HALVES)]
         ident = keep.tile([P, P], F32, name="ident")
 
-        nc.vector.memset(tab_plane[:, : T // 8], 0)
-        nc.gpsimd.memset(tab_plane[:, T // 8 :], 0)
+        nc.vector.memset(tab_plane[:], 0)
         nc.vector.memset(w_plane[:], 0)
         nc.vector.memset(wd8_plane[:], 0)
         nc.vector.memset(wd4_plane[:], 0)
-        make_identity(nc, ident[:])
+        nc.vector.memset(ident[:], 0.0)
+        make_identity(nc, ident[:], nomemset=True)
 
         wc_rows = wc.rearrange("(p i) r -> p i r", i=PACK)
         nc.sync.dma_start(offsets[:], offs)
+        load_words(nc, wd4_w, wd4_words[0])
         load_plane(nc, tab_plane, tab_scales[0])
         load_words(nc, tab_w, tab_words[0].rearrange("p t i -> p (t i)"))
         nc.sync.dma_start(out=c_raw[:], in_=c.rearrange("(p i) j -> p i j", i=PACK))
@@ -107,7 +108,6 @@ def tile_list_pnet_mix_none_kernel(
         load_words(nc, w_w, w_bytes)
         nc.sync.dma_start(out=wc_raw[0][:], in_=wc_rows[:, :, :BANK])
         nc.sync.dma_start(out=wc_raw[1][:], in_=wc_rows[:, :, BANK:])
-        load_words(nc, wd4_w, wd4_words[0])
         load_words(nc, wd8_w, wd8_words[0].rearrange("p n i -> p (n i)"))
         load_plane(nc, wd4_plane, wd4_scales[0])
         load_plane(nc, wd8_plane, wd8_scales[0])

@@ -48,11 +48,8 @@ TURN_LAG_GPSIMD = 10
 
 
 def load_plane(nc, plane, rows):
-    for quadrant in range(4):
-        nc.sync.dma_start(
-            out=plane[32 * quadrant : 32 * quadrant + 4, :],
-            in_=rows[4 * quadrant : 4 * quadrant + 4, :].bitcast(I32),
-        )
+    for r in range(4):
+        nc.sync.dma_start(out=plane[r:P:32, :], in_=rows[r:16:4, :].bitcast(I32))
 
 
 def load_words(nc, tile, words):

from contextlib import ExitStack

import concourse.mybir as mybir
from concourse.masks import make_identity

K, R, N, T, J, G = 512, 1024, 256, 2048, 512, 4
FLOPS = 2 * K * R * J * (G + 1) + 2 * R * N * J

F32 = mybir.dt.float32
BF16 = mybir.dt.bfloat16
I32 = mybir.dt.int32
U32 = mybir.dt.uint32
U16 = mybir.dt.uint16
U8 = mybir.dt.uint8
FP8X4 = mybir.dt.float8_e4m3fn_x4
FP4X4 = mybir.dt.float4_e2m1fn_x4
ALU = mybir.AluOpType
ACT = mybir.ActivationFunctionType

P = 128
PACK = 4
BANK = 512
POINT_TILES = J // P
HALVES = R // BANK
PAIRS = G // 2
PAIR_COLS = 2 * J // 16
ALIGN = 256
BANKS_A_SET = 4

RANKED = ((0, 0), (0, 1), (0, 2), (1, 0), (1, 1), (1, 2), (1, 3))
IN_EACH_SUM = (0, 3)
ON_GPSIMD = RANKED[1:-2]
LAST_SUM_APART = ON_GPSIMD[-1]
ADDED_ON_VECTOR = ()
Y_ON_VECTOR = ()
AS_PAIRS = (IN_EACH_SUM, *ON_GPSIMD, *ADDED_ON_VECTOR)
GPSIMD_COLUMNS = 256
GPSIMD_FIRST = 128
GATED_FIRST = ((RANKED[3], 1), (RANKED[0], 2), (RANKED[1], 2), (RANKED[2], 2))
ON_VECTOR = (IN_EACH_SUM,)
GATED = ((RANKED[2], 3), (RANKED[3], 2), (RANKED[4], 1))

FIRST_LEAD = 8
EACH_SUM_STEP = 5
LAST_SUM_LAG = 3
TURN_LAG = BANKS_A_SET + 1
TURN_LAG_GPSIMD = 10


def load_plane(nc, plane, rows):
    for r in range(4):
        nc.sync.dma_start(out=plane[r:P:32, :], in_=rows[r:16:4, :].bitcast(I32))


def load_words(nc, tile, words):
    nc.sync.dma_start(out=tile[:].bitcast(I32), in_=words.bitcast(I32))


def tile_list_pnet_mix_none_kernel(
    tc, tab_words, tab_scales, c, w_words, w_scales, wc, wd8_words, wd8_scales, wd4_words, wd4_scales, offs, out
):
    nc = tc.nc
    with ExitStack() as ctx:
        keep = ctx.enter_context(tc.tile_pool(name="keep", bufs=1))
        shared = ctx.enter_context(tc.tile_pool(name="shared", bufs=1))
        psum = ctx.enter_context(tc.psum_pool(name="psum", bufs=1))

        banks = [psum.tile([P, BANK], F32, name=f"bank{b}") for b in range(2 * BANKS_A_SET)]
        bank_sets = {"scalar": banks[:BANKS_A_SET], "vector": banks[BANKS_A_SET:]}
        taken = {"scalar": [], "vector": []}

        def next_bank(which):
            bank = bank_sets[which][len(taken[which]) % BANKS_A_SET]
            taken[which].append(bank)
            return bank

        offsets = keep.tile([P, PAIRS * PAIR_COLS], U16, name="offsets")
        tab_plane = keep.tile([P, T // 4], I32, name="tab_plane", align_bytes=ALIGN)
        w_plane = keep.tile([P, R // 4], I32, name="w_plane", align_bytes=ALIGN)
        wd8_plane = keep.tile([P, N // 4], I32, name="wd8_plane", align_bytes=ALIGN)
        wd4_plane = keep.tile([P, N // 4], I32, name="wd4_plane", align_bytes=ALIGN)
        tab_w = keep.tile([P, T], U32, name="tab_w", align_bytes=ALIGN)
        w_w = keep.tile([P, R], U32, name="w_w", align_bytes=ALIGN)
        wd8_w = keep.tile([P, N], U32, name="wd8_w", align_bytes=ALIGN)
        wd4_w = keep.tile([P, 2 * N], U8, name="wd4_w", align_bytes=ALIGN)
        c_raw = keep.tile([P, PACK, J], F32, name="c_raw")
        wc_raw = [shared.tile([P, PACK, BANK], F32, name=f"wc_raw{h}", offset=8192 * h) for h in range(HALVES)]
        ident = keep.tile([P, P], F32, name="ident")

        nc.vector.memset(tab_plane[:], 0)
        nc.vector.memset(w_plane[:], 0)
        nc.vector.memset(wd8_plane[:], 0)
        nc.vector.memset(wd4_plane[:], 0)
        nc.vector.memset(ident[:], 0.0)
        make_identity(nc, ident[:], nomemset=True)

        wc_rows = wc.rearrange("(p i) r -> p i r", i=PACK)
        nc.sync.dma_start(offsets[:], offs)
        load_words(nc, wd4_w, wd4_words[0])
        load_plane(nc, tab_plane, tab_scales[0])
        load_words(nc, tab_w, tab_words[0].rearrange("p t i -> p (t i)"))
        nc.sync.dma_start(out=c_raw[:], in_=c.rearrange("(p i) j -> p i j", i=PACK))
        load_plane(nc, w_plane, w_scales[0])
        w_bytes = w_words[0].rearrange("p r i -> p (r i)")
        load_words(nc, w_w, w_bytes)
        nc.sync.dma_start(out=wc_raw[0][:], in_=wc_rows[:, :, :BANK])
        nc.sync.dma_start(out=wc_raw[1][:], in_=wc_rows[:, :, BANK:])
        load_words(nc, wd8_w, wd8_words[0].rearrange("p n i -> p (n i)"))
        load_plane(nc, wd4_plane, wd4_scales[0])
        load_plane(nc, wd8_plane, wd8_scales[0])

        nb_first = [keep.tile([P, J], U32, name=f"nb_first{g}", align_bytes=ALIGN) for g in range(2)]
        nb_last = keep.tile([P, 2 * J], U32, name="nb_last", align_bytes=ALIGN)
        nb_w = [nb_first[0][:], nb_first[1][:], nb_last[:, :J], nb_last[:, J:]]
        nb_plane = [keep.tile([P, 2 * J], U8, name=f"nb_plane{pair}", align_bytes=ALIGN) for pair in range(PAIRS)]
        entries = [offsets[:, pair * PAIR_COLS : (pair + 1) * PAIR_COLS] for pair in range(PAIRS)]

        c_w = keep.tile([P, J], U32, name="c_w", align_bytes=ALIGN)
        c_plane = keep.tile([P, J], U8, name="c_plane", align_bytes=ALIGN)
        wc_w = [keep.tile([P, BANK], U32, name=f"wc_w{h}", align_bytes=ALIGN) for h in range(HALVES)]
        wc_plane = [keep.tile([P, BANK], U8, name=f"wc_plane{h}", align_bytes=ALIGN) for h in range(HALVES)]
        rounded_first = shared.tile([P, (J + BANK) * PACK], BF16, name="rounded_first", align_bytes=ALIGN, offset=16384)
        wc_bf = [rounded_first[:, (J - GPSIMD_FIRST) * PACK : (J - GPSIMD_FIRST + BANK) * PACK], shared.tile([P, BANK * PACK], BF16, name="wc_bf1", align_bytes=ALIGN, offset=16384)[:]]
        c_bf = rounded_first[:, : J * PACK]

        def round_rows(rounded, raw, cols):
            nc.scalar.activation(
                rounded[:, PACK * cols.start : PACK * cols.stop].rearrange("p (a b i) -> p a i b", b=4, i=PACK),
                raw[:, :, cols].rearrange("p i (a b) -> p a i b", b=4),
                ACT.Copy,
            )

        def round_rows_on_gpsimd(rounded, raw, cols):
            nc.gpsimd.tensor_scalar(
                rounded[:, PACK * cols.start : PACK * cols.stop].rearrange("p (a i) -> p a i", i=PACK),
                raw[:, :, cols].rearrange("p i a -> p a i"),
                1.0,
                0.0,
                ALU.mult,
                ALU.add,
            )

        def quantise(words, plane, rounded, cols):
            nc.vector.quantize_mx(
                out=words[:, cols].bitcast(FP8X4),
                scales=plane[:, cols],
                in_=rounded[:, PACK * cols.start : PACK * cols.stop],
            )

        def from_bank(bank, u):
            if u in AS_PAIRS:
                return bank[:].rearrange("j (p a e) -> j a p e", a=2, e=2)
            return bank[:].rearrange("j (b q t) -> j b t q", q=4, t=PACK)

        def in_sbuf(columns, u):
            if u in AS_PAIRS:
                return columns.rearrange("j (a p e) -> j a p e", a=2, e=2)
            return columns.rearrange("j (t b q) -> j b t q", q=4, t=PACK)

        pooled = {u: keep.tile([P, BANK], F32, name=f"pooled{u[0]}{u[1]}") for u in RANKED}
        moves = {ug: n for n, ug in enumerate(GATED_FIRST)}
        moves.update({ug: 4 + n for n, ug in enumerate(GATED)})
        running = {(u, 0): pooled[u] for u in RANKED}
        for u in RANKED:
            for g in range(1, G):
                if (u, g) in moves:
                    running[u, g] = shared.tile([P, BANK], F32, name=f"moved{u[0]}{u[1]}{g}", offset=2048 * moves[u, g])
                else:
                    running[u, g] = running[u, g - 1]
        later = {u: running[u, G - 1] for u in RANKED}
        own = {u: keep.tile([P, BANK], F32, name=f"own{u[0]}{u[1]}") for u in RANKED}
        summed = {u: keep.tile([P, BANK], BF16, name=f"summed{u[0]}{u[1]}") for u in AS_PAIRS if u != ON_GPSIMD[0]}
        summed[ON_GPSIMD[0]] = shared.tile([P, BANK], BF16, name="summed_first", align_bytes=ALIGN, offset=16384)
        last_sum = shared.tile([P, BANK], BF16, name="last_sum", align_bytes=ALIGN, offset=24576 + 1536)
        four_sums = keep.tile([P, G, BANK], BF16, name="four_sums")
        two_sums = keep.tile([P, G // 2, BANK], BF16, name="two_sums")
        h_first = keep.tile([P, 2 * P * PACK], BF16, name="h_first", align_bytes=ALIGN)
        h_bf = {(0, 0): h_first[:, : P * PACK], (0, 1): h_first[:, P * PACK :]}
        for u in (*RANKED[2:], IN_EACH_SUM):
            h_bf[u] = keep.tile([P, P * PACK], BF16, name=f"h_bf{u[0]}{u[1]}", align_bytes=ALIGN)[:]
        h_w = [shared.tile([P, J], U32, name=f"h_w{h}", align_bytes=ALIGN, offset=24576 + 2048 * h) for h in range(HALVES)]
        h_plane = [keep.tile([P, J], U8, name=f"h_plane{h}", align_bytes=ALIGN) for h in range(HALVES)]

        def neighbour_pass(bank, u, g, start):
            h, jt = u
            picked = slice((g % 2) * J + jt * P, (g % 2) * J + (jt + 1) * P)
            nc.tensor.matmul_mx(
                out=bank[:],
                lhsT=nb_w[g][:, jt * P : (jt + 1) * P].bitcast(FP8X4),
                lhsT_scale=nb_plane[g // 2][:, picked],
                rhs=w_w[:, h * BANK : (h + 1) * BANK].bitcast(FP8X4),
                rhs_scale=w_plane[:].bitcast(U8)[:, h * BANK : (h + 1) * BANK],
                start=start,
                stop=True,
            )

        def own_pass(bank, u, stop):
            h, jt = u
            nc.tensor.matmul_mx(
                out=bank[:],
                lhsT=c_w[:, jt * P : (jt + 1) * P].bitcast(FP8X4),
                lhsT_scale=c_plane[:, jt * P : (jt + 1) * P],
                rhs=wc_w[h][:].bitcast(FP8X4),
                rhs_scale=wc_plane[h][:],
                start=True,
                stop=stop,
            )

        held = []

        def neighbour(u, g, later_on=False):
            bank = next_bank("scalar" if g == 0 else "vector")
            neighbour_pass(bank, u, g, True)
            if g == 0:
                nc.scalar.activation(in_sbuf(pooled[u][:], u), from_bank(bank, u), ACT.Copy)
            else:
                before = in_sbuf(running[u, g - 1][:], u)
                after = in_sbuf(running[u, g][:], u)
                if later_on:
                    held.append(lambda: nc.vector.tensor_tensor(after, from_bank(bank, u), before, ALU.max))
                else:
                    nc.vector.tensor_tensor(after, from_bank(bank, u), before, ALU.max)

        def neighbour_with_own_part(g):
            bank = next_bank("scalar")
            own_pass(bank, IN_EACH_SUM, False)
            neighbour_pass(bank, IN_EACH_SUM, g, False)
            nc.scalar.activation(in_sbuf(four_sums[:, g, :], IN_EACH_SUM), from_bank(bank, IN_EACH_SUM), ACT.Relu)

        def last_neighbour_with_own_part(u):
            bank = next_bank("scalar")
            own_pass(bank, u, False)
            neighbour_pass(bank, u, G - 1, False)
            nc.scalar.activation(in_sbuf(last_sum[:], u), from_bank(bank, u), ACT.Relu)

        def fold_last_sum(u):
            nc.vector.tensor_tensor(summed[u][:], summed[u][:], last_sum[:], ALU.max)

        def own_part(u):
            bank = next_bank("scalar")
            own_pass(bank, u, True)
            nc.scalar.activation(in_sbuf(own[u][:], u), from_bank(bank, u), ACT.Copy)

        def add_on_vector(u):
            bank = next_bank("vector")
            own_pass(bank, u, True)
            held.append(lambda: nc.vector.tensor_tensor(in_sbuf(summed[u][:], u), from_bank(bank, u), in_sbuf(later[u][:], u), ALU.add))

        def add_on_gpsimd(u):
            nc.gpsimd.tensor_tensor(summed[u][:], later[u][:], own[u][:], ALU.add)

        begun = {}

        def begin_turn(u):
            turned = next_bank("scalar")[:].rearrange("p (t j) -> p t j", t=PACK)
            for t in range(PACK):
                nc.tensor.matmul(
                    turned[:, t, :], own[u][:, t * P : (t + 1) * P], ident[:], start=t == 0, stop=False, is_transpose=True
                )
            begun[u] = turned

        def turn(u):
            h, jt = u
            rounded = h_bf[u].rearrange("p (j t) -> p j t", t=PACK)
            if u in begun:
                turned = begun[u]
                for t in range(PACK):
                    nc.tensor.matmul(
                        turned[:, t, :], later[u][:, t * P : (t + 1) * P], ident[:], start=False, stop=t == PACK - 1, is_transpose=True
                    )
                nc.scalar.activation(rounded, turned.rearrange("p t j -> p j t"), ACT.Relu)
                return
            if u not in AS_PAIRS:
                turned = next_bank("scalar")[:].rearrange("p (t j) -> p t j", t=PACK)
                for t in range(PACK):
                    cols = slice(t * P, (t + 1) * P)
                    for term, start in ((later[u], True), (own[u], False)):
                        nc.tensor.matmul(
                            turned[:, t, :], term[:, cols], ident[:], start=start, stop=not start, is_transpose=True
                        )
                nc.scalar.activation(rounded, turned.rearrange("p t j -> p j t"), ACT.Relu)
                return
            turned = next_bank("scalar")[:, : 2 * P].rearrange("p (a j) -> p a j", a=2)
            pairs = summed[u][:].bitcast(F32)
            for a in range(2):
                nc.tensor.transpose(turned[:, a, :], pairs[:, a * P : (a + 1) * P], ident[:])
            if u in (IN_EACH_SUM, LAST_SUM_APART):
                rounded_pairs = rounded.rearrange("p j t -> p (j t)").bitcast(F32)
                copy = nc.vector.tensor_copy if u in ON_VECTOR else nc.scalar.copy
                copy(rounded_pairs.rearrange("p (j a) -> p j a", a=2), turned.rearrange("p a j -> p j a"))
                return
            values = turned.bitcast(BF16).rearrange("p a (j e) -> p j a e", e=2)
            in_order = rounded.rearrange("p j (a e) -> p j a e", e=2)
            nc.scalar.activation(in_order, values, ACT.Relu)

        def quantise_h(h, first_tile, tiles):
            cols = slice(first_tile * P, (first_tile + tiles) * P)
            nc.vector.quantize_mx(
                out=h_w[h][:, cols].bitcast(FP8X4),
                scales=h_plane[h][:, cols],
                in_=h_first[:] if tiles == 2 else h_bf[h, first_tile],
            )

        def result_passes(y, nt, points):
            nc.tensor.matmul_mx(
                out=y,
                lhsT=wd8_w[:, nt * P : (nt + 1) * P].bitcast(FP8X4),
                lhsT_scale=wd8_plane[:].bitcast(U8)[:, nt * P : (nt + 1) * P],
                rhs=h_w[0][:, points].bitcast(FP8X4),
                rhs_scale=h_plane[0][:, points],
                start=True,
                stop=False,
            )
            nc.tensor.matmul_mx(
                out=y,
                lhsT=wd4_w[:, 2 * nt * P : 2 * (nt + 1) * P].bitcast(FP4X4),
                lhsT_scale=wd4_plane[:].bitcast(U8)[:, nt * P : (nt + 1) * P],
                rhs=h_w[1][:, points].bitcast(FP8X4),
                rhs_scale=h_plane[1][:, points],
                start=False,
                stop=True,
            )

        def second_layer(jt):
            points = slice(jt * P, (jt + 1) * P)
            y_sb = keep.tile([P, N // P, P], F32, name=f"y_sb{jt}")
            if jt < POINT_TILES - 1:
                y = next_bank("vector")[:, :N].rearrange("n (nt j) -> n nt j", j=P)
                for nt in range(N // P):
                    result_passes(y[:, nt, :], nt, points)
                if jt in Y_ON_VECTOR:
                    nc.vector.tensor_copy(y_sb[:], y)
                else:
                    nc.scalar.activation(y_sb[:], y, ACT.Copy)
                nc.sync.dma_start(out=out[:, points].rearrange("(nt n) j -> n nt j", n=P), in_=y_sb[:])
                return
            upper = next_bank("vector")[:, :P]
            result_passes(upper, 0, points)
            lower = next_bank("vector")[:, :P]
            result_passes(lower, 1, points)
            nc.vector.tensor_copy(y_sb[:, 0, :], upper)
            nc.sync.dma_start(out=out[:P, points], in_=y_sb[:, 0, :])
            nc.scalar.activation(y_sb[:, 1, :], lower, ACT.Copy)
            nc.scalar.dma_start(out=out[P:, points], in_=y_sb[:, 1, :])

        whole = slice(0, BANK)
        for pair in range(PAIRS):
            nc.vector.tensor_copy(nb_plane[pair][:], tab_plane[:].bitcast(U8).indirect(entries[pair]))
        for g in range(2):
            nc.vector.tensor_copy(nb_w[g], tab_w[:].indirect(entries[0][:, g * PAIR_COLS // 2 : (g + 1) * PAIR_COLS // 2]))
        nc.vector.tensor_copy(nb_last[:], tab_w[:].indirect(entries[1]))
        round_rows(c_bf, c_raw, whole)
        quantise(c_w, c_plane, c_bf, whole)
        A, B, C, D, E, F, H = RANKED
        neighbour(A, 0)
        neighbour(B, 0)
        neighbour(C, 0)
        round_rows_on_gpsimd(wc_bf[0], wc_raw[0], slice(0, GPSIMD_FIRST))
        round_rows(wc_bf[0], wc_raw[0], slice(GPSIMD_FIRST, BANK))
        neighbour(D, 0)
        neighbour(A, 1)
        neighbour(B, 1)
        neighbour(C, 1)
        quantise(wc_w[0], wc_plane[0], wc_bf[0], whole)
        neighbour(D, 1)
        neighbour(E, 0)
        neighbour(F, 0)
        neighbour(H, 0)
        round_rows_on_gpsimd(wc_bf[1], wc_raw[1], slice(0, GPSIMD_COLUMNS))
        own_part(A)
        neighbour(A, 2)
        own_part(B)
        neighbour(B, 2)
        round_rows(wc_bf[1], wc_raw[1], slice(GPSIMD_COLUMNS, BANK))
        neighbour(A, 3)
        neighbour_with_own_part(0)
        neighbour(B, 3)
        neighbour_with_own_part(1)
        neighbour(C, 2)
        turn(A)
        quantise(wc_w[1], wc_plane[1], wc_bf[1], whole)
        add_on_gpsimd(B)
        neighbour(C, 3)
        own_part(C)
        add_on_gpsimd(C)
        neighbour(D, 2)
        neighbour(E, 1)
        own_part(D)
        neighbour(D, 3)
        add_on_gpsimd(D)
        own_part(E)
        neighbour(E, 2)
        add_on_gpsimd(E)
        neighbour(F, 1)
        neighbour_with_own_part(2)
        neighbour(H, 1)
        turn(B)
        turn(C)
        neighbour(F, 2)
        own_part(F)
        neighbour(H, 2)
        last_neighbour_with_own_part(LAST_SUM_APART)
        neighbour(F, 3)
        neighbour_with_own_part(3)
        neighbour(H, 3, later_on=True)
        own_part(H)
        turn(D)
        fold_last_sum(LAST_SUM_APART)
        turn(F)
        begin_turn(H)
        nc.vector.tensor_tensor(two_sums[:], four_sums[:, :2, :], four_sums[:, 2:, :], ALU.max)
        held.pop(0)()
        turn(E)
        nc.vector.tensor_tensor(summed[IN_EACH_SUM][:], two_sums[:, 0, :], two_sums[:, 1, :], ALU.max)
        turn(H)
        turn(IN_EACH_SUM)
        quantise_h(0, 0, 2)
        quantise_h(1, 0, 1)
        second_layer(0)
        quantise_h(0, 2, 1)
        quantise_h(1, 1, 1)
        second_layer(1)
        quantise_h(1, 2, 1)
        second_layer(2)
        quantise_h(0, 3, 1)
        quantise_h(1, 3, 1)
        second_layer(3)
